import numpy as np, ml_dtypes
CORES = [1,5,17,21,33,37,49,53]
N = 8
import mx_ref
BF = ml_dtypes.bfloat16
def gentries(a):
    return np.ascontiguousarray(a.reshape(8, 16, -1).transpose(0, 2, 1)).reshape(8, -1)
def gtable(e):
    e = np.asarray(e); return np.ascontiguousarray(e.reshape(8, -1, 16).transpose(0, 2, 1)).reshape(128, -1).astype(np.int32)
def gcols(t, e):
    v = np.concatenate([t.reshape(8, 16, -1, 4), np.zeros((8, 16, 1, 4), BF)], axis=2)
    return np.ascontiguousarray(np.stack([v[g][:, e[g]] for g in range(8)])).reshape(128, -1)
def gpick(z, e):
    return np.concatenate([z[16 * g:16 * g + 16][:, e[g]] for g in range(8)])
def pick(q, e):
    c = np.concatenate([q[0].reshape(128, -1, 4), np.zeros((128, 1, 4), np.uint8)], axis=1); s = np.concatenate([q[1], np.ones((16, 1), np.uint8)], axis=1)
    return (np.ascontiguousarray(c[:, e].reshape(128, -1)), np.ascontiguousarray(s[:, e]))
def join(*qs):
    return (np.concatenate([q[0] for q in qs], axis=1), np.concatenate([q[1] for q in qs], axis=1))
def put(q, e, v):
    c, s = q[0].reshape(128, -1, 4).copy(), q[1].copy(); c[:, e] = v[0].reshape(128, -1, 4); s[:, e] = v[1]
    return (c.reshape(128, -1), s)
def pk(c, s):
    return (np.ascontiguousarray(c), mx_ref.live(s))
def emit(q):
    return q[0], q[1]
def packed(v, rng):
    q = [mx_ref.quantize(np.ascontiguousarray(v[r])) for r in range(N)]
    return np.stack([a for a, b in q]), np.stack([mx_ref.plane(b, rng) for a, b in q])
def values_of_codes():
    e, c = np.zeros((128, 128, 4), np.float32), np.zeros((128, 2, 4), np.uint8)
    e[np.arange(128), np.arange(128), 0] = 1
    c[:127, :, 0] = np.arange(256).reshape(2, 128).T[:127]
    return mx_ref.matmul(mx_ref.quantize(e.reshape(128, 512).astype(BF)), (c.reshape(128, 8), np.full((16, 2), 127, np.uint8))).T.reshape(-1).astype(np.float64)
CODE_VALUE, SCALE_VALUE = values_of_codes(), 2.0 ** (np.arange(256) - 127.0)
def decode(q):
    return (CODE_VALUE[q[0]].reshape(16, 8, -1, 4) * SCALE_VALUE[q[1]][:, None, :, None] + 0.0).reshape(128, -1).astype(np.float32)
def f(rng, *shape):
    return mx_ref.flush((rng.standard_normal(shape, dtype=np.float32) * np.exp2(rng.integers(-2, 3, shape[:-1] + (1,)))).astype(BF))
def wide(rng, *shape, cols=0):
    v = rng.standard_normal(shape, dtype=np.float32) * np.exp2(rng.integers(-12, 13, shape)).astype(np.float32)
    if cols: v *= np.repeat(np.exp2(rng.integers(-cols, cols + 1, shape[:-2] + (1, shape[-1] // 4))) * (rng.random(shape[:-2] + (1, shape[-1] // 4)) > 0.0625), 4, axis=-1).astype(np.float32)
    return mx_ref.flush(v.astype(BF))
V, F, K, T = 512, 1024, 128, 3
def big(v, k):
    v = v.astype(np.float32) * np.float32(k)
    v[np.abs(v) < np.float32(2.0 ** -16)] = 0
    return v.astype(BF)
def weights(rng, k=1.0, still=slice(0)):
    v = big(f(rng, N, 128, 2048), k).reshape(N, 128, 4, 128, 4)
    v[:, :, :, still] = 0
    c, s = packed(v.reshape(N, 128, 2048), rng)
    return {"wc": c, "ws": s}
def lists_of(rng):
    return rng.permuted(np.tile(np.arange(F) % V, (N, 8, 1)), axis=2)
def stored(e):
    return np.stack([gtable(e[r]) for r in range(N)])
def numbers_of(rng):
    return {"x": big(f(rng, N, 128, 4 * V), 1), "fv": stored(lists_of(rng)), "u": np.array(f(rng, N, 128, 512)), "wy": np.array(f(rng, N, 128, 512))}
def planted(rng):
    at = 16 * rng.permutation(8)[:T]
    still = np.concatenate([np.arange(p, p + 16) for p in at])
    d = numbers_of(rng)
    x = d["x"].reshape(N, 128, V, 4)
    x[:, still] = 0
    d["u"][:, :, :4 * T] = 0
    d["u"][:, at, 4 * np.arange(T)] = 1
    return {**d, **weights(rng, 1.0, still)}, x, at
def setup_inputs(rng):
    return {**numbers_of(rng), **weights(rng)}
def setup_inputs_ties(rng):
    d, x, at = planted(rng)
    o = rng.permutation(N)
    none = int(rng.integers(T))
    for i in range(N):
        zero = i < N // 2
        for t in range(T):
            v = np.full(V, 0.0 if zero else 1.0, np.float32)
            j = rng.permutation(V)
            v[j[:K // 4]] = 2
            if zero: v[j[K // 4:K // 2]] = -2
            if i == 0: v *= np.float32(2.0 ** -24)
            if i == 0 and t == none: v[:] = 0
            if i == N - 1: v *= np.float32(2.0 ** 26)
            x[o[i], at[t], :, 0] = v.astype(BF)
    d["u"][o[0], at, 4 * np.arange(T)] = 2.0 ** -30
    d["u"][o[N - 1], at, 4 * np.arange(T)] = 2.0 ** 30
    return {**d, "x": x.reshape(N, 128, 4 * V)}
def setup_inputs_near(rng):
    d, x, at = planted(rng)
    e = lists_of(rng)
    sign = (rng.permutation(N) % 2 * 2.0 - 1.0).astype(np.float32).astype(BF)
    for t in range(T):
        p = int(at[t])
        e[:, p // 16] = np.arange(F) // 2
        d["u"][:, p + 1, 4 * t] = 2.0 ** 12
        d["u"][:, p + 8:p + 11, 4 * t:4 * t + 4] = 1
        x[:, p, :, 0] = sign[:, None]
        for r in range(N):
            s = np.argsort(np.argsort(np.arange(V) + 16 * rng.random(V)))
            s = (s + int(rng.integers(1, V // 4))) % V
            v = (((s[:, None] >> np.arange(12)) & 1) * np.exp2(np.arange(12) - 23.0)).astype(np.float32).astype(BF)
            x[r, p + 8:p + 11] = v.reshape(V, 3, 4).transpose(1, 0, 2)
            j = rng.permutation(V)[:8]
            x[r, p + 1, j[:4], 0] = 2.0 ** 30
            x[r, p + 1, j[4:], 0] = -2.0 ** 30
    m = int(rng.integers(N))
    later = [int(p) for p in at[1:]]
    d["u"][m, :, :4] = 0
    for p in range(0, 128, 16):
        if p in later: continue
        d["u"][m, p, 0] = 1
        d["u"][m, p + 8:p + 16, 0] = 1
        v = rng.integers(8, 16, (16, V, 4)) * rng.choice([-1.0, 1.0], (16, V, 4))
        v[:8] *= 2.0 ** -3
        v[8:] *= 2.0 ** -27
        v[0, :, 0] = 1
        x[m, p:p + 16] = v.astype(np.float32).astype(BF)
    return {**d, "x": x.reshape(N, 128, 4 * V), "fv": stored(e)}
def setup_inputs_deep(rng):
    d = numbers_of(rng)
    e = lists_of(rng)
    line = 1.0 - 2.0 * rng.integers(0, 2, (128, 4))
    sign = np.tile((rng.permutation(N) % 2 * 2.0 - 1.0)[:, None], (1, V))
    m = int(rng.permutation(np.flatnonzero(sign[:, 0] > 0))[0])
    j, k = rng.permutation(V), rng.permutation(F)
    sign[m, j[K // 4:]] = -1
    e[m][:, k[:K // 2]] = rng.permuted(np.tile(j[:K // 4], (8, 2)), axis=1)
    e[m][:, k[K // 2:]] = rng.permuted(np.tile(j[K // 4:], (8, 2)), axis=1)
    d["u"][:, :, :4 * T] = (np.tile(line, (1, T)) * 2.0 ** 30).astype(np.float32).astype(BF)
    x = np.where(rng.random((N, 128, V, 4)) < 0.0625, 0.875, 1.0) * 2.0 ** 30
    x = x * line[:, None, :] * sign[:, None, :, None]
    return {**d, "x": x.astype(np.float32).astype(BF).reshape(N, 128, 4 * V), "fv": stored(e), **weights(rng, 2.0 ** -5)}
def setup_inputs_crowd(rng):
    d, x, at = planted(rng)
    e = np.zeros((N, 8, F), int)
    for r in range(N):
        odd = bin(r).count("1") % 2
        turn = int(rng.integers(T))
        to = rng.permuted(np.tile(np.arange(V), (8, 1)), axis=1)
        e[r] = to[:, np.arange(F) % V if odd else np.arange(F) // 2]
        for t in range(T):
            v = np.ones(V, np.float32)
            if odd:
                j = 2 * rng.permutation(V // 2)[:K // 2] + rng.integers(0, 2, K // 2)
                if t == turn: j = 8 * rng.permutation(V // 8)[:K // 2] + int(rng.integers(8))
                v[j] = 64 * (1 + 0.25 * rng.integers(0, 4, K // 2))
            else:
                j = rng.permutation(V // 2)[:K // 4]
                up = rng.permutation(K // 4) % 2
                v[j + V // 2 * up] = 1024 * (1 + 0.25 * rng.integers(0, 4, K // 4))
                v[j + V // 2 * (1 - up)] = 64 * (1 + 0.25 * rng.integers(0, 4, K // 4))
            p = int(at[t])
            x[r, p, to[p // 16], 0] = v.astype(BF)
    return {**d, "x": x.reshape(N, 128, 4 * V), "fv": stored(e)}
def setup_inputs_spread(rng):
    d = setup_inputs(rng)
    d["x"] = big(wide(rng, N, 128, 4 * V, cols=6), 1)
    return d
def check_inputs(d):
    b = []
    for k in ("x", "u", "wy"):
        v = np.abs(d[k].astype(np.float32))
        if not (np.isfinite(v).all() and ((v == 0) | (v >= 2.0 ** -30) & (v <= 2.0 ** 30)).all()): b.append("a value of " + k)
    e = [gentries(a) for a in d["fv"]]
    if any(((a < 0) | (a >= V)).any() for a in e): b.append("an entry of fv out of range")
    if any((np.sort(a, axis=1) != np.arange(F) // 2).any() for a in e): b.append("a variable that isn't exactly twice in a list of fv")
    good = True
    for r in range(N):
        try:
            w = decode(pk(d["wc"][r], d["ws"][r]))
            good = good and bool(np.isfinite(w).all() and (np.abs(w) <= 2.0 ** 31).all())
        except Exception:
            good = False
    if not good: b.append("a number that wc and ws hold")
    return b
def reference(x, fv, u, wy, wc, ws):
    now = [x[r] for r in range(N)]
    e = [gentries(fv[r]) for r in range(N)]
    qu = [mx_ref.quantize(np.ascontiguousarray(u[r])) for r in range(N)]
    qw = [pk(wc[r], ws[r]) for r in range(N)]
    fl = np.zeros((N, T, K), np.float32)
    for t in range(T):
        fired, sent = [], []
        for r in range(N):
            h = mx_ref.quantize(gcols(now[r], e[r]))
            s = mx_ref.matmul(qu[r], h)[t] + np.float32(0.0)
            o = np.argsort(-s, kind="stable")[:K]
            fired.append(o)
            sent.append(pick(h, o))
            fl[r, t] = o
        new = []
        for r in range(N):
            p = r ^ (1 << t)
            low = np.full((8, V), K)
            np.minimum.at(low, (np.arange(8)[:, None], e[r][:, fired[p]]), np.tile(np.arange(K), (8, 1)))
            v = []
            for b in range(4):
                z = mx_ref.matmul(pick(qw[r], np.arange(128 * b, 128 * b + 128)), sent[p]) * np.float32(0.03125)
                v.append(gpick(np.concatenate([z, np.zeros((128, 1), np.float32)], axis=1), low))
            v = np.stack(v, axis=2).reshape(128, -1)
            hit = np.repeat(np.repeat(low < K, 16, axis=0), 4, axis=1)
            a = now[r].astype(np.float32)
            new.append(np.where(hit, a * np.float32(0.5) + v * np.float32(0.5), a).astype(BF))
        now = new
    y = np.zeros((N, 128, V), np.float32)
    oc, osc = np.zeros((N, 128, 4 * V), np.uint8), np.zeros((N, 16, V), np.uint8)
    for r in range(N):
        q = mx_ref.quantize(np.ascontiguousarray(now[r]))
        y[r] = mx_ref.matmul(mx_ref.quantize(np.ascontiguousarray(wy[r])), q)
        oc[r], osc[r] = emit(q)
    return {"y": y, "oc": oc, "osc": osc, "fl": fl}

@@ -1,0 +1,388 @@
+from concourse.bass import DstId, RemoteDMATransfer
+from concourse.mybir import dt, AluOpType, AxisListType, ActivationFunctionType
+
+ROUNDS = 3
+VCH = (3, 4, 5, 6, 7)
+SCH = (0, 1, 2)
+
+F32, BF, I32, U16, CODE, U8 = "float32", "bfloat16", "int32", "uint16", "float8_e4m3fn_x4", "uint8"
+SCRATCH = {
+    "X": ("sbuf", [128, 2560], BF), "H": ("sbuf", [128, 4096], BF),
+    "WQ": ("sbuf", [128, 512], CODE), "WSC": ("sbuf", [128, 512], U8),
+    "UB": ("sbuf", [128, 512], BF), "QU": ("sbuf", [128, 128], CODE), "SU": ("sbuf", [128, 128], U8),
+    "WYB": ("sbuf", [128, 512], BF), "QWY": ("sbuf", [128, 128], CODE), "SWY": ("sbuf", [128, 128], U8),
+    "QX": ("sbuf", [128, 512], CODE), "SX": ("sbuf", [128, 512], U8),
+    "FVT": ("sbuf", [128, 64], I32), "OFH": ("sbuf", [128, 256], U16),
+    "FVP": ("sbuf", [128, 1024], I32), "POSL": ("sbuf", [128, 64], U16), "FVN": ("sbuf", [128, 1024], F32),
+    "CC": ("sbuf", [128, 8], F32), "NCC": ("sbuf", [128, 4], F32),
+    "EQR": ("sbuf", [128, 1024], BF), "SCB": ("sbuf", [128, 2880], "float16"), "JNK": ("sbuf", [128, 1160], BF),
+    "ASU": ("sbuf", [128, 4], F32), "APR": ("sbuf", [128, 4], F32), "RK": ("sbuf", [128, 8], F32),
+    "OFR": ("sbuf", [128, 8], U16), "WIN": ("sbuf", [128, 1024], F32), "T1": ("sbuf", [128, 128], F32),
+    "TT": ("sbuf", [128, 4], F32), "TU": ("sbuf", [128, 2], F32), "T2IN": ("sbuf", [128, 64], F32),
+    "T2": ("sbuf", [128, 64], F32), "BB": ("sbuf", [128, 256], F32), "BM": ("sbuf", [128, 256], F32),
+    "PW": ("sbuf", [128, 4], F32), "PI": ("sbuf", [128, 4], I32), "F8": ("sbuf", [128, 8], I32),
+    "P32": ("sbuf", [128, 1], I32), "GI": ("sbuf", [128, 1], I32), "QI": ("sbuf", [128, 1], I32),
+    "GF": ("sbuf", [128, 1], F32), "QF": ("sbuf", [128, 1], F32), "Q4": ("sbuf", [128, 1], F32), "Q64": ("sbuf", [128, 1], F32),
+    "IV0": ("sbuf", [128, 128], F32), "IV": ("sbuf", [128, 128], F32),
+    "M40": ("sbuf", [128, 256], F32), "M4": ("sbuf", [128, 256], F32),
+    "MD0": ("sbuf", [128, 128], F32), "MD": ("sbuf", [128, 128], F32), "KROW": ("sbuf", [128, 128], F32),
+    "KW0": ("sbuf", [128, 8], F32), "KW": ("sbuf", [128, 8], F32),
+    "DM0": ("sbuf", [128, 8], F32), "DM4": ("sbuf", [128, 8], F32), "PL0": ("sbuf", [128, 64], F32),
+    "VR": ("sbuf", [128, 128], F32), "KEY": ("sbuf", [128, 128], F32), "VM": ("sbuf", [128, 128], F32),
+    "A1": ("sbuf", [128, 64], F32), "A2": ("sbuf", [128, 32], F32), "A3": ("sbuf", [128, 16], F32),
+    "VW": ("sbuf", [128, 8], F32), "NB": ("sbuf", [128, 8], F32), "VD": ("sbuf", [128, 8], F32),
+    "DB": ("sbuf", [128, 1024], BF), "SCM": ("sbuf", [128, 512], BF), "WF": ("sbuf", [128, 8], F32),
+    "WD": ("sbuf", [128, 8], F32), "VE": ("sbuf", [128, 8], F32),
+    "OFG": ("sbuf", [128, 32], U16), "OFS": ("sbuf", [128, 32], U16),
+    "OLD": ("sbuf", [128, 512], F32), "TMP": ("sbuf", [128, 512], F32), "NV": ("sbuf", [128, 512], BF),
+    "YS": ("sbuf", [128, 512], F32),
+    "psR": ("psum", [128, 2048], F32), "psC": ("psum", [128, 2048], F32),
+}
+for _c in VCH:
+    SCRATCH["CB%d" % _c] = ("sbuf", [128, 1152], BF)
+for _c in SCH:
+    SCRATCH["SG%d" % _c] = ("sbuf", [128, 1160], BF)
+for _t in range(ROUNDS):
+    SCRATCH["UO%d" % _t] = ("sbuf", [128, 8], U16)
+    SCRATCH["QUR%d" % _t] = ("sbuf", [128, 128], CODE)
+    SCRATCH["SUR%d" % _t] = ("sbuf", [128, 128], U8)
+    SCRATCH["QH%d" % _t] = ("sbuf", [128, 1024], CODE)
+    SCRATCH["SH%d" % _t] = ("sbuf", [128, 1024], U8)
+    SCRATCH["SL%d" % _t] = ("sbuf", [128, 128], CODE)
+    SCRATCH["SS%d" % _t] = ("sbuf", [128, 128], U8)
+    SCRATCH["LC%d" % _t] = ("sbuf", [128, 128], CODE)
+    SCRATCH["LS%d" % _t] = ("sbuf", [128, 128], U8)
+    SCRATCH["LR%d" % _t] = ("sbuf", [128, 8], U16)
+    SCRATCH["LST%d" % _t] = ("sbuf", [128, 8], U16)
+    SCRATCH["FLS%d" % _t] = ("sbuf", [128, 8], F32)
+
+SEMAPHORES = ["cv", "cs", "ct", "cg", "dx", "dfv", "du", "dfp", "dw", "dwy", "dout", "sent"]
+for _t in range(ROUNDS):
+    SEMAPHORES += ["arrL%d" % _t, "arrC%d" % _t, "arrS%d" % _t]
+
+
+def rank_program(g, core, T, topo):
+    rank = T.rank_of(core)
+    if rank is None:
+        return
+    A, ACT, AX = AluOpType, ActivationFunctionType, AxisListType
+    V, S, TE, SY = g.vector, g.scalar, g.tensor, g.sync
+    queue = {"v": V, "s": S, "t": TE, "g": g, "y": SY}
+    own = {"v": "cv", "s": "cs", "t": "ct", "g": "cg"}
+
+    count = {k: 0 for k in own}
+    known = {k: {} for k in queue}
+    most, total = {}, {}
+    wr, rd = {}, {}
+
+    def need(e, tok):
+        sem, n = tok
+        if known[e].get(sem, 0) < n:
+            queue[e].wait_ge(T.sem[sem], n)
+            known[e][sem] = n
+            most[sem] = max(most.get(sem, 0), n)
+
+    def deps(e, reads, writes):
+        want = {}
+        for n, a, b in reads:
+            for (x, y, tok, w) in wr.get(n, []):
+                if x < b and a < y:
+                    want[tok[0]] = max(want.get(tok[0], 0), tok[1])
+        for n, a, b in writes:
+            for (x, y, tok, w) in wr.get(n, []):
+                if x < b and a < y:
+                    want[tok[0]] = max(want.get(tok[0], 0), tok[1])
+            for (x, y, tok, w) in rd.get(n, []):
+                if x < b and a < y and w != e:
+                    want[tok[0]] = max(want.get(tok[0], 0), tok[1])
+        for sem in sorted(want):
+            need(e, (sem, want[sem]))
+
+    def note(e, tok, reads, writes):
+        for n, a, b in writes:
+            wr[n] = [r for r in wr.get(n, []) if not (a <= r[0] and r[1] <= b)] + [(a, b, tok, e)]
+            rd[n] = [r for r in rd.get(n, []) if not (a <= r[0] and r[1] <= b)]
+        for n, a, b in reads:
+            rd[n] = [r for r in rd.get(n, []) if not (r[3] == e and a <= r[0] and r[1] <= b)] + [(a, b, tok, e)]
+
+    def op(e, call, reads, writes):
+        deps(e, reads, writes)
+        count[e] += 1
+        total[own[e]] = count[e]
+        call().then_inc(T.sem[own[e]], 1)
+        note(e, (own[e], count[e]), reads, writes)
+
+    def dma(e, out, in_, sem, n, reads, writes):
+        deps(e, reads, writes)
+        total[sem] = total.get(sem, 0) + 16
+        queue[e].dma_start(out, in_).then_inc(T.sem[sem], 16)
+        note("d" + sem, (sem, 16 * n), reads, writes)
+
+    def ts(out, in0, s1, s2, *ops):
+        return lambda: V.tensor_scalar(out, in0, s1, s2, *ops)
+
+    def tt(out, a, b, o):
+        return lambda: V.tensor_tensor(out, a, b, o)
+
+    def cp(out, in_):
+        return lambda: V.tensor_copy(out, in_)
+
+    def ms(ap, c):
+        return lambda: V.memset(ap, c)
+
+    def act(out, in_, func, **kw):
+        return lambda: S.activation(out, in_, func, **kw)
+
+    def mm(out, a, sa, b, sb):
+        return lambda: TE.matmul_mx(out, a, sa, b, sb, True, True)
+
+    def iota(name, pattern, base, cm, n):
+        flag = SCRATCH[name][2] != I32
+        if flag:
+            op("g", lambda: g.iota(T[name][:], pattern, base, cm, allow_small_or_imprecise_dtypes=True), [], [(name, 0, n)])
+        else:
+            op("g", lambda: g.iota(T[name][:], pattern, base, cm), [], [(name, 0, n)])
+
+    dma("y", T.X[:, 0:2048], T.x[:], "dx", 1, [], [("X", 0, 2048)])
+    dma("s", T.FVT[:], T.fv[:], "dfv", 1, [], [("FVT", 0, 64)])
+    dma("s", T.UB[:], T.u[:], "du", 1, [], [("UB", 0, 512)])
+    need("y", ("dx", 16))
+    dma("y", T.WQ[:, 0:512].bitcast(dt.uint8), T.wc[:], "dw", 2, [], [("WQ", 0, 512)])
+    dma("y", T.WSC[:, 0:512], T.ws[:], "dw", 2, [], [("WSC", 0, 512)])
+    for q in range(16):
+        dma("y", T.FVP[q:128:16, :], T.fv[:], "dfp", 16, [], [("FVP.%d" % q, 0, 1024)])
+    dma("y", T.WYB[:], T.wy[:], "dwy", 1, [], [("WYB", 0, 512)])
+
+    iota("P32", [[0, 1]], 0, 1, 1)
+    iota("IV0", [[128, 8], [1, 16]], 0, 0, 128)
+    iota("M40", [[0, 4], [1, 16], [0, 4]], 0, 0, 256)
+    iota("MD0", [[0, 8], [1, 16]], 0, 0, 128)
+    iota("KROW", [[64, 2], [1, 4], [4, 16]], 0, 0, 128)
+    iota("KW0", [[64, 2], [1, 4]], 0, 0, 8)
+    iota("DM0", [[64, 8]], 2048, 0, 8)
+    iota("PL0", [[1, 64]], 0, 0, 64)
+    for e in range(4):
+        op("v", ts(T.OFH[:, 64 * e:64 * e + 64], T.FVT[:], 4.0, float(e), A.mult, A.add), [("FVT", 0, 64)], [("OFH", 64 * e, 64 * e + 64)])
+    op("v", ts(T.GI[:], T.P32[:], 4, None, A.arith_shift_right), [("P32", 0, 1)], [("GI", 0, 1)])
+    op("v", ts(T.QI[:], T.P32[:], 15, None, A.bitwise_and), [("P32", 0, 1)], [("QI", 0, 1)])
+    op("v", ts(T.GF[:], T.GI[:], 16.0, None, A.mult), [("GI", 0, 1)], [("GF", 0, 1)])
+    op("v", cp(T.QF[:], T.QI[:]), [("QI", 0, 1)], [("QF", 0, 1)])
+    op("v", ts(T.Q4[:], T.QI[:], 4.0, None, A.mult), [("QI", 0, 1)], [("Q4", 0, 1)])
+    op("v", ts(T.Q64[:], T.QI[:], 64.0, None, A.mult), [("QI", 0, 1)], [("Q64", 0, 1)])
+    op("v", lambda: V.quantize_mx(T.QU[:, 0:128], T.SU[:, 0:128], T.UB[:, 0:512]), [("UB", 0, 512)], [("QU", 0, 128), ("SU", 0, 128)])
+    for t in range(ROUNDS):
+        op("v", ms(T["UO%d" % t][:], t), [], [("UO%d" % t, 0, 8)])
+        off = T["UO%d" % t]
+        op("v", cp(T["QUR%d" % t][:, 0:128].bitcast(dt.uint32), T.QU[:, 0:128].bitcast(dt.uint32).indirect(off[:, 0:8])),
+           [("QU", 0, 128), ("UO%d" % t, 0, 8)], [("QUR%d" % t, 0, 128)])
+        op("v", cp(T["SUR%d" % t][:, 0:128], T.SU[:, 0:128].indirect(off[:, 0:8])),
+           [("SU", 0, 128), ("UO%d" % t, 0, 8)], [("SUR%d" % t, 0, 128)])
+    op("v", ms(T.APR[:], 0.0), [], [("APR", 0, 4)])
+    for c in SCH:
+        op("v", ms(T["SG%d" % c][:, 1152:1160], float(128 * c)), [], [("SG%d" % c, 1152, 1160)])
+    op("v", ms(T.T2IN[:], 0.0), [], [("T2IN", 0, 64)])
+    op("v", ts(T.IV[:], T.IV0[:], T.GF[:, 0:1], None, A.add), [("IV0", 0, 128), ("GF", 0, 1)], [("IV", 0, 128)])
+    op("v", ts(T.M4[:], T.M40[:], T.QF[:, 0:1], None, A.is_equal), [("M40", 0, 256), ("QF", 0, 1)], [("M4", 0, 256)])
+    op("v", ts(T.MD[:], T.MD0[:], T.QF[:, 0:1], None, A.is_equal), [("MD0", 0, 128), ("QF", 0, 1)], [("MD", 0, 128)])
+    op("v", ts(T.KW[:], T.KW0[:], T.Q4[:, 0:1], None, A.add), [("KW0", 0, 8), ("Q4", 0, 1)], [("KW", 0, 8)])
+    op("v", ts(T.DM4[:], T.DM0[:], T.Q4[:, 0:1], None, A.add), [("DM0", 0, 8), ("Q4", 0, 1)], [("DM4", 0, 8)])
+    op("v", ts(T.POSL[:], T.PL0[:], T.Q64[:, 0:1], None, A.add), [("PL0", 0, 64), ("Q64", 0, 1)], [("POSL", 0, 64)])
+
+    partners = [T.cores[rank ^ (1 << t)] for t in range(ROUNDS)]
+    common = [e for e in topo.engines(core, partners[0]) if all(e in topo.engines(core, p) for p in partners)]
+    mask, ne = sum(1 << e for e in common), len(common)
+
+    def send(t, land, src, arr, reads):
+        deps("g", reads, [])
+        rid, pid = topo.addr(partners[t])[:2]
+        total["sent"] = total.get("sent", 0) + ne
+        g.remote_dma(land, src, T.sem[arr], T.sem.sent, pid, rid, mask)
+        total[arr] = ne
+
+    def gather(e, el, lo, hi):
+        out = T.H[:, 4 * lo + el:4 * hi:4]
+        win = T.X[:, 0:2048].indirect(T.OFH[:, 64 * el + lo // 16:64 * el + hi // 16])
+        reads = [("X", 0, 2048), ("OFH", 64 * el, 64 * el + 64)]
+        writes = [("H.%d" % el, lo, hi)]
+        if e == "v":
+            op("v", cp(out, win), reads, writes)
+        else:
+            op("s", act(out, win, ACT.Copy), reads, writes)
+
+    for t in range(ROUNDS):
+        QH, SH, QUR, SUR = T["QH%d" % t], T["SH%d" % t], T["QUR%d" % t], T["SUR%d" % t]
+        nQH, nSH = "QH%d" % t, "SH%d" % t
+        ru = [("QUR%d" % t, 0, 128), ("SUR%d" % t, 0, 128)]
+
+        def quant(h):
+            op("v", lambda: V.quantize_mx(QH[:, 512 * h:512 * h + 512], SH[:, 512 * h:512 * h + 512], T.H[:, 2048 * h:2048 * h + 2048]),
+               [("H.%d" % e, 512 * h, 512 * h + 512) for e in range(4)], [(nQH, 512 * h, 512 * h + 512), (nSH, 512 * h, 512 * h + 512)])
+
+        def rows(h, base):
+            a = 512 * h
+            op("t", mm(T.psR[:, base + a:base + a + 512], QUR[:, 0:128], SUR[:, 0:128], QH[:, a:a + 512], SH[:, a:a + 512]),
+               ru + [(nQH, a, a + 512), (nSH, a, a + 512)], [("psR", base + a, base + a + 512)])
+
+        def cols(c):
+            k = c % 4
+            op("t", mm(T.psC[:, 512 * k:512 * k + 128], QH[:, 128 * c:128 * c + 128], SH[:, 128 * c:128 * c + 128], QUR[:, 0:128], SUR[:, 0:128]),
+               ru + [(nQH, 128 * c, 128 * c + 128), (nSH, 128 * c, 128 * c + 128)], [("psC", 512 * k, 512 * k + 512)])
+
+        gather("v", 0, 0, 512)
+        gather("s", 2, 0, 512)
+        gather("v", 1, 0, 512)
+        gather("s", 3, 0, 512)
+        quant(0)
+        gather("s", 2, 512, 1024)
+        gather("s", 3, 512, 1024)
+        gather("v", 0, 512, 1024)
+        gather("s", 1, 768, 1024)
+        gather("v", 1, 512, 768)
+        for c in range(4):
+            cols(c)
+        rows(0, 0)
+        rows(0, 1024)
+        quant(1)
+        rows(1, 0)
+        rows(1, 1024)
+
+        def eq(c):
+            op("v", ts(T.EQR[:, 128 * c:128 * c + 128], T.psR[:, 128 * c:128 * c + 128], T.CC[:, c:c + 1], None, A.is_equal),
+               [("psR", 128 * c, 128 * c + 128), ("CC", c, c + 1)], [("EQR", 128 * c, 128 * c + 128)])
+            dst, nm = (T["SG%d" % c], "SG%d" % c) if c in SCH else (T["CB%d" % c], "CB%d" % c)
+            op("g", lambda: g.affine_select(dst[:, 1024:1152], T.EQR[:, 128 * c:128 * c + 128], [[-1, 128]], A.is_gt, 0.0, 0, 1),
+               [("EQR", 128 * c, 128 * c + 128)], [(nm, 1024, 1152)])
+
+        def beat(c, a, b, o):
+            op("v", ts(T["CB%d" % c][:, a:b], T.psR[:, a:b], T.CC[:, c:c + 1], None, o),
+               [("psR", a, b), ("CC", c, c + 1)], [("CB%d" % c, a, b)])
+
+        def total_of(i, c):
+            cb = T["CB%d" % c]
+            op("v", lambda: V.tensor_tensor_scan(T.SCB[:, 576 * i:576 * i + 576], cb[:, 0:576], cb[:, 576:1152], 0.0, A.add, A.add),
+               [("CB%d" % c, 0, 1152)], [("SCB", 576 * i, 576 * i + 576)])
+
+        op("v", cp(T.CC[:, 0:4], T.psC[:, 0:2048:512]), [("psC", 0, 2048)], [("CC", 0, 4)])
+        for c in range(4, 8):
+            cols(c)
+        op("v", ts(T.NCC[:, 0:3], T.CC[:, 0:3], -1.0, None, A.mult), [("CC", 0, 3)], [("NCC", 0, 3)])
+        for c in range(4):
+            eq(c)
+        op("v", ms(T.WIN[:, 0:128], 0.0), [], [("WIN", 0, 128)])
+        for c in SCH:
+            sg, nm = T["SG%d" % c], "SG%d" % c
+            op("s", act(sg[:, 0:1024], T.psR[:, 1024:2048], ACT.Sign, bias=T.NCC[:, c:c + 1]),
+               [("psR", 1024, 2048), ("NCC", c, c + 1)], [(nm, 0, 1024)])
+            if c:
+                op("s", act(T.JNK[:, 0:128 * c], sg[:, 0:128 * c], ACT.Relu, scale=-1.0, accum_out=T.APR[:, c:c + 1]),
+                   [(nm, 0, 128 * c)], [("APR", c, c + 1), ("JNK", 0, 1160)])
+            op("s", act(T.JNK[:, 128 * c:1153], sg[:, 128 * c:1153], ACT.Relu, accum_out=T.ASU[:, c:c + 1]),
+               [(nm, 128 * c, 1160)], [("ASU", c, c + 1), ("JNK", 0, 1160)])
+        for i, c in enumerate(VCH):
+            if c >= 4:
+                if c == 4:
+                    op("v", cp(T.CC[:, 4:8], T.psC[:, 0:2048:512]), [("psC", 0, 2048)], [("CC", 4, 8)])
+                eq(c)
+            beat(c, 0, 128 * c, A.is_ge)
+            beat(c, 128 * c, 1024, A.is_gt)
+            if i:
+                total_of(i - 1, VCH[i - 1])
+        total_of(len(VCH) - 1, VCH[-1])
+        op("v", cp(T.RK[:, 3:8], T.SCB[:, 575:2880:576]), [("SCB", 0, 2880)], [("RK", 3, 8)])
+        op("v", tt(T.RK[:, 0:3], T.ASU[:, 0:3], T.APR[:, 0:3], A.subtract), [("ASU", 0, 3), ("APR", 0, 3)], [("RK", 0, 3)])
+        op("v", cp(T.OFR[:], T.RK[:]), [("RK", 0, 8)], [("OFR", 0, 8)])
+        op("v", cp(T.WIN[:, 0:1024].indirect(T.OFR[:, 0:8]), T.IV[:]), [("OFR", 0, 8), ("IV", 0, 128)], [("WIN", 0, 1024)])
+        op("v", lambda: V.transpose(T.T1[:], T.WIN[:, 0:128]), [("WIN", 0, 128)], [("T1", 0, 128)])
+        op("v", tt(T.TT[:], T.T1[:, 0:128:32], T.T1[:, 16:128:32], A.add), [("T1", 0, 128)], [("TT", 0, 4)])
+        op("v", ts(T.TU[:], T.TT[:, 0:2], 1024.0, None, A.mult), [("TT", 0, 4)], [("TU", 0, 2)])
+        op("v", tt(T.T2IN[:, 0:64:32], T.TU[:], T.TT[:, 2:4], A.add), [("TT", 0, 4), ("TU", 0, 2)], [("T2IN", 0, 64)])
+        op("v", lambda: V.transpose(T.T2[:], T.T2IN[:]), [("T2IN", 0, 64)], [("T2", 0, 64)])
+        for a in range(4):
+            op("g", lambda: g.partition_broadcast(T.BB[:, 64 * a:64 * a + 64], T.T2[32 * a:32 * a + 1, 0:64], 128),
+               [("T2", 0, 64)], [("BB", 64 * a, 64 * a + 64)])
+        if t == 0:
+            op("v", ts(T.FVN[:], T.FVP[:].indirect(T.POSL[:, 0:64]), 256.0, None, A.mult),
+               [("FVP.%d" % q, 0, 1024) for q in range(16)] + [("POSL", 0, 64)], [("FVN", 0, 1024)])
+        op("v", tt(T.BM[:], T.BB[:], T.M4[:], A.mult), [("BB", 0, 256), ("M4", 0, 256)], [("BM", 0, 256)])
+        for m in range(4):
+            op("v", lambda: V.tensor_reduce(T.PW[:, m:m + 1], T.BM[:, m:256:4], AX.X, A.add), [("BM", 0, 256)], [("PW", m, m + 1)])
+        op("v", cp(T.PI[:], T.PW[:]), [("PW", 0, 4)], [("PI", 0, 4)])
+        op("v", ts(T.F8[:, 0:4], T.PI[:], 10, None, A.arith_shift_right), [("PI", 0, 4)], [("F8", 0, 4)])
+        op("v", ts(T.F8[:, 4:8], T.PI[:], 1023, None, A.bitwise_and), [("PI", 0, 4)], [("F8", 4, 8)])
+        LST, nL = T["LST%d" % t], "LST%d" % t
+        op("v", cp(LST[:], T.F8[:]), [("F8", 0, 8)], [(nL, 0, 8)])
+
+        send(t, T["LR%d" % t][:], LST[:], "arrL%d" % t, [(nL, 0, 8)])
+        op("v", cp(T["SL%d" % t][:, 0:128].bitcast(dt.uint32), QH[:, 0:1024].bitcast(dt.uint32).indirect(LST[:, 0:8])),
+           [(nQH, 0, 1024), (nL, 0, 8)], [("SL%d" % t, 0, 128)])
+        op("s", act(T["SS%d" % t][:, 0:128], SH[:, 0:1024].indirect(LST[:, 0:8]), ACT.Copy),
+           [(nSH, 0, 1024), (nL, 0, 8)], [("SS%d" % t, 0, 128)])
+        send(t, T["LC%d" % t][:, 0:128].bitcast(dt.uint8), T["SL%d" % t][:, 0:128].bitcast(dt.uint8), "arrC%d" % t, [("SL%d" % t, 0, 128)])
+        send(t, T["LS%d" % t][:, 0:128], T["SS%d" % t][:, 0:128], "arrS%d" % t, [("SS%d" % t, 0, 128)])
+        note("a", ("arrL%d" % t, ne), [], [("LR%d" % t, 0, 8)])
+        note("a", ("arrC%d" % t, ne), [], [("LC%d" % t, 0, 128)])
+        note("a", ("arrS%d" % t, ne), [], [("LS%d" % t, 0, 128)])
+        FLS, nF = T["FLS%d" % t], "FLS%d" % t
+        op("v", cp(FLS[:], T.F8[:]), [("F8", 0, 8)], [(nF, 0, 8)])
+        nout = 2 * ROUNDS + 7
+        dma("y", T.fl[t:t + 1, 0:64], FLS[0:16, 0:4], "dout", nout, [(nF, 0, 8)], [])
+        dma("y", T.fl[t:t + 1, 64:128], FLS[0:16, 4:8], "dout", nout, [(nF, 0, 8)], [])
+        if t == 0:
+            op("v", lambda: V.quantize_mx(T.QWY[:, 0:128], T.SWY[:, 0:128], T.WYB[:, 0:512]), [("WYB", 0, 512)], [("QWY", 0, 128), ("SWY", 0, 128)])
+
+        LR = T["LR%d" % t]
+        op("v", cp(T.VR[:], T.FVN[:].indirect(LR[:, 0:8])), [("FVN", 0, 1024), ("LR%d" % t, 0, 8)], [("VR", 0, 128)])
+        op("v", tt(T.VM[:], T.VR[:], T.MD[:], A.mult), [("VR", 0, 128), ("MD", 0, 128)], [("VM", 0, 128)])
+        op("v", tt(T.KEY[:], T.VR[:], T.KROW[:], A.add), [("VR", 0, 128), ("KROW", 0, 128)], [("KEY", 0, 128)])
+        op("v", tt(T.A1[:], T.VM[:, 0:128:2], T.VM[:, 1:128:2], A.add), [("VM", 0, 128)], [("A1", 0, 64)])
+        op("v", tt(T.A2[:], T.A1[:, 0:64:2], T.A1[:, 1:64:2], A.add), [("A1", 0, 64)], [("A2", 0, 32)])
+        op("v", tt(T.A3[:], T.A2[:, 0:32:2], T.A2[:, 1:32:2], A.add), [("A2", 0, 32)], [("A3", 0, 16)])
+        op("v", tt(T.VW[:], T.A3[:, 0:16:2], T.A3[:, 1:16:2], A.add), [("A3", 0, 16)], [("VW", 0, 8)])
+        op("v", ts(T.NB[:], T.VW[:], -1.0, None, A.mult), [("VW", 0, 8)], [("NB", 0, 8)])
+        for m in range(8):
+            op("s", act(T.DB[:, 128 * m:128 * m + 128], T.KEY[:], ACT.Abs, bias=T.NB[:, m:m + 1]),
+               [("KEY", 0, 128), ("NB", 0, 8)], [("DB", 128 * m, 128 * m + 128)])
+        for e in range(4):
+            op("v", ts(T.OFG[:, 8 * e:8 * e + 8], T.VW[:], 1.0 / 64, float(e), A.mult, A.add), [("VW", 0, 8)], [("OFG", 8 * e, 8 * e + 8)])
+        op("v", ts(T.OLD[:], T.X[:, 0:2048].indirect(T.OFG[:, 0:32]), 32.0, None, A.mult),
+           [("X", 0, 2048), ("OFG", 0, 32)], [("OLD", 0, 512)])
+        op("v", ts(T.VD[:], T.VW[:], 1.0 / 64, None, A.mult), [("VW", 0, 8)], [("VD", 0, 8)])
+        op("v", tt(T.VE[:], T.VD[:], T.DM4[:], A.subtract), [("VD", 0, 8), ("DM4", 0, 8)], [("VE", 0, 8)])
+        for m in range(8):
+            a = 128 * m
+            op("v", lambda: V.tensor_tensor_scan(T.SCM[:, 64 * m:64 * m + 64], T.DB[:, a:a + 64], T.DB[:, a + 64:a + 128], 30000.0, A.min, A.min),
+               [("DB", a, a + 128)], [("SCM", 64 * m, 64 * m + 64)])
+        op("v", tt(T.WF[:], T.SCM[:, 63:512:64], T.KW[:], A.is_equal), [("SCM", 0, 512), ("KW", 0, 8)], [("WF", 0, 8)])
+        op("v", tt(T.WD[:], T.VE[:], T.WF[:], A.mult), [("VE", 0, 8), ("WF", 0, 8)], [("WD", 0, 8)])
+        op("v", tt(T.VD[:], T.WD[:], T.DM4[:], A.add), [("WD", 0, 8), ("DM4", 0, 8)], [("VD", 0, 8)])
+        for e in range(4):
+            op("v", ts(T.OFS[:, 8 * e:8 * e + 8], T.VD[:], float(e), None, A.add), [("VD", 0, 8)], [("OFS", 8 * e, 8 * e + 8)])
+
+        for b in range(4):
+            op("t", mm(T.psC[:, 512 * b:512 * b + 128], T.WQ[:, 128 * b:128 * b + 128], T.WSC[:, 128 * b:128 * b + 128],
+                       T["LC%d" % t][:, 0:128], T["LS%d" % t][:, 0:128]),
+               [("WQ", 0, 512), ("WSC", 0, 512), ("LC%d" % t, 0, 128), ("LS%d" % t, 0, 128)], [("psC", 512 * b, 512 * b + 512)])
+        for b in range(4):
+            a = 128 * b
+            op("v", tt(T.TMP[:, a:a + 128], T.psC[:, 512 * b:512 * b + 128], T.OLD[:, a:a + 128], A.add),
+               [("psC", 512 * b, 512 * b + 128), ("OLD", a, a + 128)], [("TMP", a, a + 128)])
+            op("s", act(T.NV[:, a:a + 128], T.TMP[:, a:a + 128], ACT.Copy, scale=1.0 / 64), [("TMP", a, a + 128)], [("NV", a, a + 128)])
+        for b in range(2):
+            op("v", cp(T.X[:, 0:2560].indirect(T.OFS[:, 16 * b:16 * b + 16]), T.NV[:, 256 * b:256 * b + 256]),
+               [("OFS", 0, 32), ("NV", 256 * b, 256 * b + 256)], [("X", 0, 2560)])
+
+    op("v", lambda: V.quantize_mx(T.QX[:, 0:512], T.SX[:, 0:512], T.X[:, 0:2048]), [("X", 0, 2048)], [("QX", 0, 512), ("SX", 0, 512)])
+    nout = 2 * ROUNDS + 7
+    for h in range(2):
+        op("t", mm(T.psR[:, 1024 * h:1024 * h + 256], T.QWY[:, 0:128], T.SWY[:, 0:128], T.QX[:, 256 * h:256 * h + 256], T.SX[:, 256 * h:256 * h + 256]),
+           [("QWY", 0, 128), ("SWY", 0, 128), ("QX", 0, 512), ("SX", 0, 512)], [("psR", 1024 * h, 1024 * h + 512)])
+    dma("y", T.oc[:, 0:2048], T.QX[:, 0:512].bitcast(dt.uint8), "dout", nout, [("QX", 0, 512)], [])
+    op("v", cp(T.YS[:, 0:256], T.psR[:, 0:256]), [("psR", 0, 256)], [("YS", 0, 256)])
+    op("s", act(T.YS[:, 256:512], T.psR[:, 1024:1280], ACT.Copy), [("psR", 1024, 1280)], [("YS", 256, 512)])
+    dma("s", T.y[:, 256:512], T.YS[:, 256:512], "dout", nout, [("YS", 256, 512)], [])
+    dma("y", T.y[:, 0:256], T.YS[:, 0:256], "dout", nout, [("YS", 0, 256)], [])
+    for k in range(4):
+        dma("s" if k % 2 else "y", T.osc[4 * k:4 * k + 4, :], T.SX[32 * k:32 * k + 4, 0:512], "dout", nout, [("SX", 0, 512)], [])
+    for sem in sorted(total):
+        if most.get(sem, 0) < total[sem]:
+            need("g", (sem, total[sem]))

@@ -2,42 +2,41 @@ from concourse.bass import DstId, RemoteDMATransfer
 from concourse.mybir import dt, AluOpType, AxisListType, ActivationFunctionType
 
 ROUNDS = 3
-VCH = (3, 4, 5, 6, 7)
-SCH = (0, 1, 2)
+VCH = (2, 3, 4, 5, 6)
+SCH = (0, 1, 7)
 
-F32, BF, I32, U16, CODE, U8 = "float32", "bfloat16", "int32", "uint16", "float8_e4m3fn_x4", "uint8"
+F32, BF, F16, I32, U16, CODE, U8 = "float32", "bfloat16", "float16", "int32", "uint16", "float8_e4m3fn_x4", "uint8"
 SCRATCH = {
-    "X": ("sbuf", [128, 2560], BF), "H": ("sbuf", [128, 4096], BF),
+    "XI": ("sbuf", [128, 2048], BF), "XF": ("sbuf", [128, 2048], BF), "H": ("sbuf", [128, 4096], BF),
     "WQ": ("sbuf", [128, 512], CODE), "WSC": ("sbuf", [128, 512], U8),
     "UB": ("sbuf", [128, 512], BF), "QU": ("sbuf", [128, 128], CODE), "SU": ("sbuf", [128, 128], U8),
     "WYB": ("sbuf", [128, 512], BF), "QWY": ("sbuf", [128, 128], CODE), "SWY": ("sbuf", [128, 128], U8),
     "QX": ("sbuf", [128, 512], CODE), "SX": ("sbuf", [128, 512], U8),
-    "FVT": ("sbuf", [128, 64], I32), "OFH": ("sbuf", [128, 256], U16),
+    "FVT": ("sbuf", [128, 64], I32), "OFH": ("sbuf", [128, 256], U16), "OFP": ("sbuf", [128, 64], U16),
     "FVP": ("sbuf", [128, 1024], I32), "POSL": ("sbuf", [128, 64], U16), "FVN": ("sbuf", [128, 1024], F32),
     "CC": ("sbuf", [128, 8], F32), "NCC": ("sbuf", [128, 4], F32),
-    "EQR": ("sbuf", [128, 1024], BF), "SCB": ("sbuf", [128, 2880], "float16"), "JNK": ("sbuf", [128, 1160], BF),
+    "EQR": ("sbuf", [128, 1024], BF), "SCB": ("sbuf", [128, 2880], F16), "JNK": ("sbuf", [128, 3480], BF),
     "ASU": ("sbuf", [128, 4], F32), "APR": ("sbuf", [128, 4], F32), "RK": ("sbuf", [128, 8], F32),
     "OFR": ("sbuf", [128, 8], U16), "WIN": ("sbuf", [128, 1024], F32), "T1": ("sbuf", [128, 128], F32),
-    "TT": ("sbuf", [128, 4], F32), "TU": ("sbuf", [128, 2], F32), "T2IN": ("sbuf", [128, 64], F32),
-    "T2": ("sbuf", [128, 64], F32), "BB": ("sbuf", [128, 256], F32), "BM": ("sbuf", [128, 256], F32),
+    "PK": ("sbuf", [128, 8], F32), "T2IN": ("sbuf", [128, 96], F32), "T2": ("sbuf", [128, 64], F32),
+    "BB": ("sbuf", [128, 256], F32), "BM": ("sbuf", [128, 256], F32),
     "PW": ("sbuf", [128, 4], F32), "PI": ("sbuf", [128, 4], I32), "F8": ("sbuf", [128, 8], I32),
     "P32": ("sbuf", [128, 1], I32), "GI": ("sbuf", [128, 1], I32), "QI": ("sbuf", [128, 1], I32),
-    "GF": ("sbuf", [128, 1], F32), "QF": ("sbuf", [128, 1], F32), "Q4": ("sbuf", [128, 1], F32), "Q64": ("sbuf", [128, 1], F32),
+    "GF": ("sbuf", [128, 1], F32), "QF": ("sbuf", [128, 1], F32), "Q64": ("sbuf", [128, 1], F32),
     "IV0": ("sbuf", [128, 128], F32), "IV": ("sbuf", [128, 128], F32),
-    "M40": ("sbuf", [128, 256], F32), "M4": ("sbuf", [128, 256], F32),
-    "MD0": ("sbuf", [128, 128], F32), "MD": ("sbuf", [128, 128], F32), "KROW": ("sbuf", [128, 128], F32),
-    "KW0": ("sbuf", [128, 8], F32), "KW": ("sbuf", [128, 8], F32),
-    "DM0": ("sbuf", [128, 8], F32), "DM4": ("sbuf", [128, 8], F32), "PL0": ("sbuf", [128, 64], F32),
-    "VR": ("sbuf", [128, 128], F32), "KEY": ("sbuf", [128, 128], F32), "VM": ("sbuf", [128, 128], F32),
-    "A1": ("sbuf", [128, 64], F32), "A2": ("sbuf", [128, 32], F32), "A3": ("sbuf", [128, 16], F32),
-    "VW": ("sbuf", [128, 8], F32), "NB": ("sbuf", [128, 8], F32), "VD": ("sbuf", [128, 8], F32),
-    "DB": ("sbuf", [128, 1024], BF), "SCM": ("sbuf", [128, 512], BF), "WF": ("sbuf", [128, 8], F32),
-    "WD": ("sbuf", [128, 8], F32), "VE": ("sbuf", [128, 8], F32),
-    "OFG": ("sbuf", [128, 32], U16), "OFS": ("sbuf", [128, 32], U16),
+    "MD0": ("sbuf", [128, 128], F32), "MD": ("sbuf", [128, 128], F32),
+    "KM0": ("sbuf", [128, 1024], F32), "KM": ("sbuf", [128, 1024], F16), "IOT": ("sbuf", [128, 1024], F32),
+    "RV0": ("sbuf", [128, 8], F32), "REV": ("sbuf", [128, 8], U16), "PL0": ("sbuf", [128, 64], F32),
+    "VRO": ("sbuf", [128, 128], F16), "VM": ("sbuf", [128, 128], F32), "ZR": ("sbuf", [128, 128], F32),
+    "VC": ("sbuf", [128, 144], F32), "VW": ("sbuf", [128, 8], F32), "EQ": ("sbuf", [128, 1024], F16),
+    "LOS": ("sbuf", [128, 1024], F16), "VD": ("sbuf", [128, 8], F32),
+    "OFG": ("sbuf", [128, 8], U16), "OFS": ("sbuf", [128, 8], U16), "FR": ("sbuf", [128, 128], F32),
     "OLD": ("sbuf", [128, 512], F32), "TMP": ("sbuf", [128, 512], F32), "NV": ("sbuf", [128, 512], BF),
     "YS": ("sbuf", [128, 512], F32),
     "psR": ("psum", [128, 2048], F32), "psC": ("psum", [128, 2048], F32),
 }
+for _e in range(4):
+    SCRATCH["XP%d" % _e] = ("sbuf", [128, 1024], BF)
 for _c in VCH:
     SCRATCH["CB%d" % _c] = ("sbuf", [128, 1152], BF)
 for _c in SCH:
@@ -54,7 +53,7 @@ for _t in range(ROUNDS):
     SCRATCH["LS%d" % _t] = ("sbuf", [128, 128], U8)
     SCRATCH["LR%d" % _t] = ("sbuf", [128, 8], U16)
     SCRATCH["LST%d" % _t] = ("sbuf", [128, 8], U16)
-    SCRATCH["FLS%d" % _t] = ("sbuf", [128, 8], F32)
+    SCRATCH["FLS%d" % _t] = ("sbuf", [128, 128], F32)
 
 SEMAPHORES = ["cv", "cs", "ct", "cg", "dx", "dfv", "du", "dfp", "dw", "dwy", "dout", "sent"]
 for _t in range(ROUNDS):
@@ -124,6 +123,9 @@ def rank_program(g, core, T, topo):
     def tt(out, a, b, o):
         return lambda: V.tensor_tensor(out, a, b, o)
 
+    def scan(out, a, b, o0, o1):
+        return lambda: V.tensor_tensor_scan(out, a, b, 0.0, o0, o1)
+
     def cp(out, in_):
         return lambda: V.tensor_copy(out, in_)
 
@@ -137,13 +139,12 @@ def rank_program(g, core, T, topo):
         return lambda: TE.matmul_mx(out, a, sa, b, sb, True, True)
 
     def iota(name, pattern, base, cm, n):
-        flag = SCRATCH[name][2] != I32
-        if flag:
+        if SCRATCH[name][2] != I32:
             op("g", lambda: g.iota(T[name][:], pattern, base, cm, allow_small_or_imprecise_dtypes=True), [], [(name, 0, n)])
         else:
             op("g", lambda: g.iota(T[name][:], pattern, base, cm), [], [(name, 0, n)])
 
-    dma("y", T.X[:, 0:2048], T.x[:], "dx", 1, [], [("X", 0, 2048)])
+    dma("y", T.XI[:], T.x[:], "dx", 1, [], [("XI", 0, 2048)])
     dma("s", T.FVT[:], T.fv[:], "dfv", 1, [], [("FVT", 0, 64)])
     dma("s", T.UB[:], T.u[:], "du", 1, [], [("UB", 0, 512)])
     need("y", ("dx", 16))
@@ -155,42 +156,46 @@ def rank_program(g, core, T, topo):
 
     iota("P32", [[0, 1]], 0, 1, 1)
     iota("IV0", [[128, 8], [1, 16]], 0, 0, 128)
-    iota("M40", [[0, 4], [1, 16], [0, 4]], 0, 0, 256)
     iota("MD0", [[0, 8], [1, 16]], 0, 0, 128)
-    iota("KROW", [[64, 2], [1, 4], [4, 16]], 0, 0, 128)
-    iota("KW0", [[64, 2], [1, 4]], 0, 0, 8)
-    iota("DM0", [[64, 8]], 2048, 0, 8)
     iota("PL0", [[1, 64]], 0, 0, 64)
+    iota("RV0", [[-16, 8]], 127, 0, 8)
+    iota("KM0", [[-16, 8], [1, 128]], 0, 0, 1024)
+    iota("IOT", [[1, 1024]], 0, 0, 1024)
     for e in range(4):
         op("v", ts(T.OFH[:, 64 * e:64 * e + 64], T.FVT[:], 4.0, float(e), A.mult, A.add), [("FVT", 0, 64)], [("OFH", 64 * e, 64 * e + 64)])
+    op("v", cp(T.OFP[:], T.FVT[:]), [("FVT", 0, 64)], [("OFP", 0, 64)])
     op("v", ts(T.GI[:], T.P32[:], 4, None, A.arith_shift_right), [("P32", 0, 1)], [("GI", 0, 1)])
     op("v", ts(T.QI[:], T.P32[:], 15, None, A.bitwise_and), [("P32", 0, 1)], [("QI", 0, 1)])
     op("v", ts(T.GF[:], T.GI[:], 16.0, None, A.mult), [("GI", 0, 1)], [("GF", 0, 1)])
     op("v", cp(T.QF[:], T.QI[:]), [("QI", 0, 1)], [("QF", 0, 1)])
-    op("v", ts(T.Q4[:], T.QI[:], 4.0, None, A.mult), [("QI", 0, 1)], [("Q4", 0, 1)])
     op("v", ts(T.Q64[:], T.QI[:], 64.0, None, A.mult), [("QI", 0, 1)], [("Q64", 0, 1)])
     op("v", lambda: V.quantize_mx(T.QU[:, 0:128], T.SU[:, 0:128], T.UB[:, 0:512]), [("UB", 0, 512)], [("QU", 0, 128), ("SU", 0, 128)])
-    for t in range(ROUNDS):
+
+    def lay_u(t):
         op("v", ms(T["UO%d" % t][:], t), [], [("UO%d" % t, 0, 8)])
         off = T["UO%d" % t]
         op("v", cp(T["QUR%d" % t][:, 0:128].bitcast(dt.uint32), T.QU[:, 0:128].bitcast(dt.uint32).indirect(off[:, 0:8])),
            [("QU", 0, 128), ("UO%d" % t, 0, 8)], [("QUR%d" % t, 0, 128)])
         op("v", cp(T["SUR%d" % t][:, 0:128], T.SU[:, 0:128].indirect(off[:, 0:8])),
            [("SU", 0, 128), ("UO%d" % t, 0, 8)], [("SUR%d" % t, 0, 128)])
-    op("v", ms(T.APR[:], 0.0), [], [("APR", 0, 4)])
+
+    lay_u(0)
+    op("v", ms(T.PK[:], 1.0), [], [("PK", 0, 8)])
     for c in SCH:
-        op("v", ms(T["SG%d" % c][:, 1152:1160], float(128 * c)), [], [("SG%d" % c, 1152, 1160)])
-    op("v", ms(T.T2IN[:], 0.0), [], [("T2IN", 0, 64)])
+        op("v", ms(T["SG%d" % c][:, 6:7], float(128 * c - 896)), [], [("SG%d" % c, 6, 7)])
+        op("v", ts(T["SG%d" % c][:, 7:8], T.P32[:], -127.0, None, A.add), [("P32", 0, 1)], [("SG%d" % c, 7, 8)])
+    op("v", ms(T.T2IN[:], 0.0), [], [("T2IN", 0, 96)])
+    op("v", ms(T.PK[:, 0:8:4], 0.0), [], [("PK", 0, 8)])
     op("v", ts(T.IV[:], T.IV0[:], T.GF[:, 0:1], None, A.add), [("IV0", 0, 128), ("GF", 0, 1)], [("IV", 0, 128)])
-    op("v", ts(T.M4[:], T.M40[:], T.QF[:, 0:1], None, A.is_equal), [("M40", 0, 256), ("QF", 0, 1)], [("M4", 0, 256)])
+    op("v", ms(T.PK[:, 2:8:4], 1024.0), [], [("PK", 0, 8)])
     op("v", ts(T.MD[:], T.MD0[:], T.QF[:, 0:1], None, A.is_equal), [("MD0", 0, 128), ("QF", 0, 1)], [("MD", 0, 128)])
-    op("v", ts(T.KW[:], T.KW0[:], T.Q4[:, 0:1], None, A.add), [("KW0", 0, 8), ("Q4", 0, 1)], [("KW", 0, 8)])
-    op("v", ts(T.DM4[:], T.DM0[:], T.Q4[:, 0:1], None, A.add), [("DM0", 0, 8), ("Q4", 0, 1)], [("DM4", 0, 8)])
     op("v", ts(T.POSL[:], T.PL0[:], T.Q64[:, 0:1], None, A.add), [("PL0", 0, 64), ("Q64", 0, 1)], [("POSL", 0, 64)])
+    op("v", ts(T.REV[:], T.RV0[:], T.QF[:, 0:1], None, A.subtract), [("RV0", 0, 8), ("QF", 0, 1)], [("REV", 0, 8)])
 
     partners = [T.cores[rank ^ (1 << t)] for t in range(ROUNDS)]
     common = [e for e in topo.engines(core, partners[0]) if all(e in topo.engines(core, p) for p in partners)]
     mask, ne = sum(1 << e for e in common), len(common)
+    nout = ROUNDS + 7
 
     def send(t, land, src, arr, reads):
         deps("g", reads, [])
@@ -199,24 +204,24 @@ def rank_program(g, core, T, topo):
         g.remote_dma(land, src, T.sem[arr], T.sem.sent, pid, rid, mask)
         total[arr] = ne
 
-    def gather(e, el, lo, hi):
-        out = T.H[:, 4 * lo + el:4 * hi:4]
-        win = T.X[:, 0:2048].indirect(T.OFH[:, 64 * el + lo // 16:64 * el + hi // 16])
-        reads = [("X", 0, 2048), ("OFH", 64 * el, 64 * el + 64)]
-        writes = [("H.%d" % el, lo, hi)]
-        if e == "v":
-            op("v", cp(out, win), reads, writes)
-        else:
-            op("s", act(out, win, ACT.Copy), reads, writes)
-
     for t in range(ROUNDS):
         QH, SH, QUR, SUR = T["QH%d" % t], T["SH%d" % t], T["QUR%d" % t], T["SUR%d" % t]
         nQH, nSH = "QH%d" % t, "SH%d" % t
         ru = [("QUR%d" % t, 0, 128), ("SUR%d" % t, 0, 128)]
 
-        def quant(h):
-            op("v", lambda: V.quantize_mx(QH[:, 512 * h:512 * h + 512], SH[:, 512 * h:512 * h + 512], T.H[:, 2048 * h:2048 * h + 2048]),
-               [("H.%d" % e, 512 * h, 512 * h + 512) for e in range(4)], [(nQH, 512 * h, 512 * h + 512), (nSH, 512 * h, 512 * h + 512)])
+        def gather(e, el, lo, hi):
+            out = T.H[:, 4 * lo + el:4 * hi:4]
+            if t == 0:
+                win = T.XI[:, 0:2048].indirect(T.OFH[:, 64 * el + lo // 16:64 * el + hi // 16])
+                reads = [("XI", 0, 2048), ("OFH", 64 * el, 64 * el + 64)]
+            else:
+                win = T["XP%d" % el][:, 0:512].indirect(T.OFP[:, lo // 16:hi // 16])
+                reads = [("XP%d" % el, 0, 512), ("OFP", 0, 64)]
+            op(e, cp(out, win) if e == "v" else act(out, win, ACT.Copy), reads, [("H.%d" % el, lo, hi)])
+
+        def quant(a, b):
+            op("v", lambda: V.quantize_mx(QH[:, a:b], SH[:, a:b], T.H[:, 4 * a:4 * b]),
+               [("H.%d" % e, a, b) for e in range(4)], [(nQH, a, b), (nSH, a, b)])
 
         def rows(h, base):
             a = 512 * h
@@ -228,87 +233,115 @@ def rank_program(g, core, T, topo):
             op("t", mm(T.psC[:, 512 * k:512 * k + 128], QH[:, 128 * c:128 * c + 128], SH[:, 128 * c:128 * c + 128], QUR[:, 0:128], SUR[:, 0:128]),
                ru + [(nQH, 128 * c, 128 * c + 128), (nSH, 128 * c, 128 * c + 128)], [("psC", 512 * k, 512 * k + 512)])
 
-        gather("v", 0, 0, 512)
-        gather("s", 2, 0, 512)
-        gather("v", 1, 0, 512)
-        gather("s", 3, 0, 512)
-        quant(0)
-        gather("s", 2, 512, 1024)
-        gather("s", 3, 512, 1024)
-        gather("v", 0, 512, 1024)
-        gather("s", 1, 768, 1024)
-        gather("v", 1, 512, 768)
+        if t == 0:
+            first = [("v", 0), ("s", 2), ("v", 1), ("s", 3)]
+            second = [("s", 2, 512, 1024), ("s", 3, 512, 1024), ("v", 0, 512, 1024), ("s", 1, 768, 1024), ("v", 1, 512, 768)]
+        else:
+            first = [("s", 0), ("s", 1), ("v", 2), ("v", 3)]
+            second = [("s", 0, 512, 1024), ("s", 1, 512, 1024), ("s", 2, 512, 1024), ("v", 3, 512, 768), ("s", 3, 768, 1024)]
+        for e, el in first:
+            gather(e, el, 0, 512)
+        quant(0, 512)
+        for e, el, lo, hi in second:
+            gather(e, el, lo, hi)
         for c in range(4):
             cols(c)
+        quant(512, 768)
+        quant(768, 1024)
         rows(0, 0)
         rows(0, 1024)
-        quant(1)
+        op("v", cp(T.CC[:, 0:4], T.psC[:, 0:2048:512]), [("psC", 0, 2048)], [("CC", 0, 4)])
+        op("v", ts(T.NCC[:, 0:2], T.CC[:, 0:2], -1.0, None, A.mult), [("CC", 0, 2)], [("NCC", 0, 2)])
         rows(1, 0)
+        for c in range(4, 8):
+            cols(c)
         rows(1, 1024)
 
+        def sign(i, h):
+            c = SCH[i]
+            op("s", act(T["SG%d" % c][:, 8 + 512 * h:520 + 512 * h], T.psR[:, 1024 + 512 * h:1536 + 512 * h], ACT.Sign, bias=T.NCC[:, i:i + 1]),
+               [("psR", 1024 + 512 * h, 1536 + 512 * h), ("NCC", i, i + 1)], [("SG%d" % c, 8 + 512 * h, 520 + 512 * h)])
+
+        def triangles(i):
+            c = SCH[i]
+            sg, nm, d = T["SG%d" % c], "SG%d" % c, 8 + 128 * c
+            op("g", lambda: g.affine_select(sg[:, 1032:1160], sg[:, d:d + 128], [[1, 128]], A.is_gt, 0.0, 0, -1),
+               [(nm, d, d + 128)], [(nm, 1032, 1160)])
+            op("g", lambda: g.affine_select(sg[:, d:d + 128], sg[:, d:d + 128], [[-1, 128]], A.is_gt, 0.0, 0, 1),
+               [(nm, d, d + 128)], [(nm, d, d + 128)])
+
         def eq(c):
+            cb = T["CB%d" % c]
             op("v", ts(T.EQR[:, 128 * c:128 * c + 128], T.psR[:, 128 * c:128 * c + 128], T.CC[:, c:c + 1], None, A.is_equal),
                [("psR", 128 * c, 128 * c + 128), ("CC", c, c + 1)], [("EQR", 128 * c, 128 * c + 128)])
-            dst, nm = (T["SG%d" % c], "SG%d" % c) if c in SCH else (T["CB%d" % c], "CB%d" % c)
-            op("g", lambda: g.affine_select(dst[:, 1024:1152], T.EQR[:, 128 * c:128 * c + 128], [[-1, 128]], A.is_gt, 0.0, 0, 1),
-               [("EQR", 128 * c, 128 * c + 128)], [(nm, 1024, 1152)])
+            op("g", lambda: g.affine_select(cb[:, 1024:1152], T.EQR[:, 128 * c:128 * c + 128], [[1, 128]], A.is_gt, 0.0, 0, -1),
+               [("EQR", 128 * c, 128 * c + 128)], [("CB%d" % c, 1024, 1152)])
 
         def beat(c, a, b, o):
             op("v", ts(T["CB%d" % c][:, a:b], T.psR[:, a:b], T.CC[:, c:c + 1], None, o),
                [("psR", a, b), ("CC", c, c + 1)], [("CB%d" % c, a, b)])
 
-        def total_of(i, c):
-            cb = T["CB%d" % c]
-            op("v", lambda: V.tensor_tensor_scan(T.SCB[:, 576 * i:576 * i + 576], cb[:, 0:576], cb[:, 576:1152], 0.0, A.add, A.add),
-               [("CB%d" % c, 0, 1152)], [("SCB", 576 * i, 576 * i + 576)])
+        def total_of(i):
+            cb = T["CB%d" % VCH[i]]
+            op("v", scan(T.SCB[:, 576 * i:576 * i + 576], cb[:, 0:576], cb[:, 576:1152], A.add, A.add),
+               [("CB%d" % VCH[i], 0, 1152)], [("SCB", 576 * i, 576 * i + 576)])
 
-        op("v", cp(T.CC[:, 0:4], T.psC[:, 0:2048:512]), [("psC", 0, 2048)], [("CC", 0, 4)])
-        for c in range(4, 8):
-            cols(c)
-        op("v", ts(T.NCC[:, 0:3], T.CC[:, 0:3], -1.0, None, A.mult), [("CC", 0, 3)], [("NCC", 0, 3)])
-        for c in range(4):
+        for i in (0, 1):
+            sign(i, 0)
+            triangles(i)
+        for c in (2, 3):
             eq(c)
-        op("v", ms(T.WIN[:, 0:128], 0.0), [], [("WIN", 0, 128)])
-        for c in SCH:
-            sg, nm = T["SG%d" % c], "SG%d" % c
-            op("s", act(sg[:, 0:1024], T.psR[:, 1024:2048], ACT.Sign, bias=T.NCC[:, c:c + 1]),
-               [("psR", 1024, 2048), ("NCC", c, c + 1)], [(nm, 0, 1024)])
-            if c:
-                op("s", act(T.JNK[:, 0:128 * c], sg[:, 0:128 * c], ACT.Relu, scale=-1.0, accum_out=T.APR[:, c:c + 1]),
-                   [(nm, 0, 128 * c)], [("APR", c, c + 1), ("JNK", 0, 1160)])
-            op("s", act(T.JNK[:, 128 * c:1153], sg[:, 128 * c:1153], ACT.Relu, accum_out=T.ASU[:, c:c + 1]),
-               [(nm, 128 * c, 1160)], [("ASU", c, c + 1), ("JNK", 0, 1160)])
-        for i, c in enumerate(VCH):
-            if c >= 4:
-                if c == 4:
-                    op("v", cp(T.CC[:, 4:8], T.psC[:, 0:2048:512]), [("psC", 0, 2048)], [("CC", 4, 8)])
+        beat(2, 0, 384, A.is_lt)
+        beat(2, 384, 512, A.is_le)
+        beat(3, 0, 512, A.is_lt)
+        op("v", ms(T.WIN[:, 896:1024], 0.0), [], [("WIN", 896, 1024)])
+        op("v", cp(T.CC[:, 4:8], T.psC[:, 0:2048:512]), [("psC", 0, 2048)], [("CC", 4, 8)])
+        op("v", ts(T.NCC[:, 2:3], T.CC[:, 7:8], -1.0, None, A.mult), [("CC", 7, 8)], [("NCC", 2, 3)])
+        for i, h in ((2, 0), (2, 1), (0, 1), (1, 1)):
+            sign(i, h)
+        triangles(2)
+        for i, c in enumerate(SCH):
+            sg, nm, d, j = T["SG%d" % c], "SG%d" % c, 136 + 128 * c, 1160 * i
+            op("s", act(T.JNK[:, j + 6:j + d], sg[:, 6:d], ACT.Relu, scale=-1.0, accum_out=T.APR[:, i:i + 1]),
+               [(nm, 6, d)], [("APR", i, i + 1), ("JNK", j + 6, j + d)])
+            op("s", act(T.JNK[:, j + d:j + 1160], sg[:, d:1160], ACT.Relu, accum_out=T.ASU[:, i:i + 1]),
+               [(nm, d, 1160)], [("ASU", i, i + 1), ("JNK", j + d, j + 1160)])
+        beat(2, 512, 1024, A.is_le)
+        eq(4)
+        beat(3, 512, 1024, A.is_le)
+        total_of(0)
+        for i in (2, 3, 4):
+            c = VCH[i]
+            if i > 2:
                 eq(c)
-            beat(c, 0, 128 * c, A.is_ge)
-            beat(c, 128 * c, 1024, A.is_gt)
-            if i:
-                total_of(i - 1, VCH[i - 1])
-        total_of(len(VCH) - 1, VCH[-1])
-        op("v", cp(T.RK[:, 3:8], T.SCB[:, 575:2880:576]), [("SCB", 0, 2880)], [("RK", 3, 8)])
-        op("v", tt(T.RK[:, 0:3], T.ASU[:, 0:3], T.APR[:, 0:3], A.subtract), [("ASU", 0, 3), ("APR", 0, 3)], [("RK", 0, 3)])
+            beat(c, 0, 128 * c + 128, A.is_lt)
+            beat(c, 128 * c + 128, 1024, A.is_le)
+            total_of(i - 1)
+        total_of(4)
+        op("v", cp(T.RK[:, 2:7], T.SCB[:, 575:2880:576]), [("SCB", 0, 2880)], [("RK", 2, 7)])
+        op("v", tt(T.RK[:, 0:2], T.APR[:, 0:2], T.ASU[:, 0:2], A.subtract), [("ASU", 0, 2), ("APR", 0, 2)], [("RK", 0, 2)])
+        op("v", tt(T.RK[:, 7:8], T.APR[:, 2:3], T.ASU[:, 2:3], A.subtract), [("ASU", 2, 3), ("APR", 2, 3)], [("RK", 7, 8)])
         op("v", cp(T.OFR[:], T.RK[:]), [("RK", 0, 8)], [("OFR", 0, 8)])
         op("v", cp(T.WIN[:, 0:1024].indirect(T.OFR[:, 0:8]), T.IV[:]), [("OFR", 0, 8), ("IV", 0, 128)], [("WIN", 0, 1024)])
-        op("v", lambda: V.transpose(T.T1[:], T.WIN[:, 0:128]), [("WIN", 0, 128)], [("T1", 0, 128)])
-        op("v", tt(T.TT[:], T.T1[:, 0:128:32], T.T1[:, 16:128:32], A.add), [("T1", 0, 128)], [("TT", 0, 4)])
-        op("v", ts(T.TU[:], T.TT[:, 0:2], 1024.0, None, A.mult), [("TT", 0, 4)], [("TU", 0, 2)])
-        op("v", tt(T.T2IN[:, 0:64:32], T.TU[:], T.TT[:, 2:4], A.add), [("TT", 0, 4), ("TU", 0, 2)], [("T2IN", 0, 64)])
-        op("v", lambda: V.transpose(T.T2[:], T.T2IN[:]), [("T2IN", 0, 64)], [("T2", 0, 64)])
+        op("v", lambda: V.transpose(T.T1[:], T.WIN[:, 896:1024]), [("WIN", 896, 1024)], [("T1", 0, 128)])
+        op("v", scan(T.T2IN[:, 8:65:8], T.PK[:], T.T1[:, 0:128:16], A.mult, A.add), [("T1", 0, 128), ("PK", 0, 8)], [("T2IN", 0, 96)])
+        op("v", lambda: V.transpose(T.T2[:], T.T2IN[:, 32:96]), [("T2IN", 0, 96)], [("T2", 0, 64)])
         for a in range(4):
             op("g", lambda: g.partition_broadcast(T.BB[:, 64 * a:64 * a + 64], T.T2[32 * a:32 * a + 1, 0:64], 128),
                [("T2", 0, 64)], [("BB", 64 * a, 64 * a + 64)])
         if t == 0:
-            op("v", ts(T.FVN[:], T.FVP[:].indirect(T.POSL[:, 0:64]), 256.0, None, A.mult),
+            op("v", cp(T.FVN[:], T.FVP[:].indirect(T.POSL[:, 0:64])),
                [("FVP.%d" % q, 0, 1024) for q in range(16)] + [("POSL", 0, 64)], [("FVN", 0, 1024)])
-        op("v", tt(T.BM[:], T.BB[:], T.M4[:], A.mult), [("BB", 0, 256), ("M4", 0, 256)], [("BM", 0, 256)])
+        for a in range(4):
+            op("v", tt(T.BM[:, a:256:4], T.BB[:, 64 * a:64 * a + 64], T.MD[:, 0:64], A.mult),
+               [("BB", 64 * a, 64 * a + 64), ("MD", 0, 128)], [("BM.%d" % a, 0, 256)])
         for m in range(4):
-            op("v", lambda: V.tensor_reduce(T.PW[:, m:m + 1], T.BM[:, m:256:4], AX.X, A.add), [("BM", 0, 256)], [("PW", m, m + 1)])
+            op("v", lambda: V.tensor_reduce(T.PW[:, m:m + 1], T.BM[:, 64 * m:64 * m + 64], AX.X, A.add),
+               [("BM.%d" % a, 0, 256) for a in range(4)], [("PW", m, m + 1)])
         op("v", cp(T.PI[:], T.PW[:]), [("PW", 0, 4)], [("PI", 0, 4)])
-        op("v", ts(T.F8[:, 0:4], T.PI[:], 10, None, A.arith_shift_right), [("PI", 0, 4)], [("F8", 0, 4)])
-        op("v", ts(T.F8[:, 4:8], T.PI[:], 1023, None, A.bitwise_and), [("PI", 0, 4)], [("F8", 4, 8)])
+        for b in range(2):
+            op("v", ts(T.F8[:, 4 * b:4 * b + 2], T.PI[:, 2 * b:2 * b + 2], 10, None, A.arith_shift_right), [("PI", 0, 4)], [("F8", 4 * b, 4 * b + 2)])
+            op("v", ts(T.F8[:, 4 * b + 2:4 * b + 4], T.PI[:, 2 * b:2 * b + 2], 1023, None, A.bitwise_and), [("PI", 0, 4)], [("F8", 4 * b + 2, 4 * b + 4)])
         LST, nL = T["LST%d" % t], "LST%d" % t
         op("v", cp(LST[:], T.F8[:]), [("F8", 0, 8)], [(nL, 0, 8)])
 
@@ -323,40 +356,36 @@ def rank_program(g, core, T, topo):
         note("a", ("arrC%d" % t, ne), [], [("LC%d" % t, 0, 128)])
         note("a", ("arrS%d" % t, ne), [], [("LS%d" % t, 0, 128)])
         FLS, nF = T["FLS%d" % t], "FLS%d" % t
-        op("v", cp(FLS[:], T.F8[:]), [("F8", 0, 8)], [(nF, 0, 8)])
-        nout = 2 * ROUNDS + 7
-        dma("y", T.fl[t:t + 1, 0:64], FLS[0:16, 0:4], "dout", nout, [(nF, 0, 8)], [])
-        dma("y", T.fl[t:t + 1, 64:128], FLS[0:16, 4:8], "dout", nout, [(nF, 0, 8)], [])
+        op("s", act(T.FR[:], T.IOT[:].indirect(LST[:, 0:8]), ACT.Copy), [("IOT", 0, 1024), (nL, 0, 8)], [("FR", 0, 128)])
+        op("s", act(FLS[:], T.FR[:].indirect(T.REV[:, 0:8]), ACT.Copy), [("FR", 0, 128), ("REV", 0, 8)], [(nF, 0, 128)])
+        dma("y", T.fl[t:t + 1, :], FLS[0:1, :], "dout", nout, [(nF, 0, 128)], [])
         if t == 0:
+            op("v", ms(T.ZR[:], 0.0), [], [("ZR", 0, 128)])
+            op("v", ms(T.VC[:, 0:16], 0.0), [], [("VC", 0, 16)])
+            op("v", ts(T.KM[:], T.KM0[:], T.QF[:, 0:1], None, A.is_gt), [("KM0", 0, 1024), ("QF", 0, 1)], [("KM", 0, 1024)])
+            lay_u(1)
+            for e in range(4):
+                op("s", act(T["XP%d" % e][:, 0:512], T.XI[:, e:2048:4], ACT.Copy), [("XI", 0, 2048)], [("XP%d" % e, 0, 512)])
+        if t == 1:
+            lay_u(2)
             op("v", lambda: V.quantize_mx(T.QWY[:, 0:128], T.SWY[:, 0:128], T.WYB[:, 0:512]), [("WYB", 0, 512)], [("QWY", 0, 128), ("SWY", 0, 128)])
 
-        LR = T["LR%d" % t]
-        op("v", cp(T.VR[:], T.FVN[:].indirect(LR[:, 0:8])), [("FVN", 0, 1024), ("LR%d" % t, 0, 8)], [("VR", 0, 128)])
-        op("v", tt(T.VM[:], T.VR[:], T.MD[:], A.mult), [("VR", 0, 128), ("MD", 0, 128)], [("VM", 0, 128)])
-        op("v", tt(T.KEY[:], T.VR[:], T.KROW[:], A.add), [("VR", 0, 128), ("KROW", 0, 128)], [("KEY", 0, 128)])
-        op("v", tt(T.A1[:], T.VM[:, 0:128:2], T.VM[:, 1:128:2], A.add), [("VM", 0, 128)], [("A1", 0, 64)])
-        op("v", tt(T.A2[:], T.A1[:, 0:64:2], T.A1[:, 1:64:2], A.add), [("A1", 0, 64)], [("A2", 0, 32)])
-        op("v", tt(T.A3[:], T.A2[:, 0:32:2], T.A2[:, 1:32:2], A.add), [("A2", 0, 32)], [("A3", 0, 16)])
-        op("v", tt(T.VW[:], T.A3[:, 0:16:2], T.A3[:, 1:16:2], A.add), [("A3", 0, 16)], [("VW", 0, 8)])
-        op("v", ts(T.NB[:], T.VW[:], -1.0, None, A.mult), [("VW", 0, 8)], [("NB", 0, 8)])
-        for m in range(8):
-            op("s", act(T.DB[:, 128 * m:128 * m + 128], T.KEY[:], ACT.Abs, bias=T.NB[:, m:m + 1]),
-               [("KEY", 0, 128), ("NB", 0, 8)], [("DB", 128 * m, 128 * m + 128)])
+        LR, nR = T["LR%d" % t], "LR%d" % t
+        op("v", tt(T.VM[:], T.FVN[:].indirect(LR[:, 0:8]), T.MD[:], A.mult), [("FVN", 0, 1024), (nR, 0, 8), ("MD", 0, 128)], [("VM", 0, 128)])
+        op("v", cp(T.VRO[:], T.FVN[:].indirect(LR[:, 0:8])), [("FVN", 0, 1024), (nR, 0, 8)], [("VRO", 0, 128)])
+        op("v", scan(T.VC[:, 16:144], T.VM[:], T.ZR[:], A.add, A.add), [("VM", 0, 128), ("ZR", 0, 128)], [("VC", 16, 144)])
+        op("v", tt(T.VW[:], T.VC[:, 31:144:16], T.VC[:, 15:128:16], A.subtract), [("VC", 0, 144)], [("VW", 0, 8)])
+        op("v", cp(T.OFG[:], T.VW[:]), [("VW", 0, 8)], [("OFG", 0, 8)])
         for e in range(4):
-            op("v", ts(T.OFG[:, 8 * e:8 * e + 8], T.VW[:], 1.0 / 64, float(e), A.mult, A.add), [("VW", 0, 8)], [("OFG", 8 * e, 8 * e + 8)])
-        op("v", ts(T.OLD[:], T.X[:, 0:2048].indirect(T.OFG[:, 0:32]), 32.0, None, A.mult),
-           [("X", 0, 2048), ("OFG", 0, 32)], [("OLD", 0, 512)])
-        op("v", ts(T.VD[:], T.VW[:], 1.0 / 64, None, A.mult), [("VW", 0, 8)], [("VD", 0, 8)])
-        op("v", tt(T.VE[:], T.VD[:], T.DM4[:], A.subtract), [("VD", 0, 8), ("DM4", 0, 8)], [("VE", 0, 8)])
+            op("s", act(T.OLD[:, 128 * e:128 * e + 128], T["XP%d" % e][:, 0:512].indirect(T.OFG[:, 0:8]), ACT.Copy, scale=32.0),
+               [("XP%d" % e, 0, 512), ("OFG", 0, 8)], [("OLD", 128 * e, 128 * e + 128)])
         for m in range(8):
             a = 128 * m
-            op("v", lambda: V.tensor_tensor_scan(T.SCM[:, 64 * m:64 * m + 64], T.DB[:, a:a + 64], T.DB[:, a + 64:a + 128], 30000.0, A.min, A.min),
-               [("DB", a, a + 128)], [("SCM", 64 * m, 64 * m + 64)])
-        op("v", tt(T.WF[:], T.SCM[:, 63:512:64], T.KW[:], A.is_equal), [("SCM", 0, 512), ("KW", 0, 8)], [("WF", 0, 8)])
-        op("v", tt(T.WD[:], T.VE[:], T.WF[:], A.mult), [("VE", 0, 8), ("WF", 0, 8)], [("WD", 0, 8)])
-        op("v", tt(T.VD[:], T.WD[:], T.DM4[:], A.add), [("WD", 0, 8), ("DM4", 0, 8)], [("VD", 0, 8)])
-        for e in range(4):
-            op("v", ts(T.OFS[:, 8 * e:8 * e + 8], T.VD[:], float(e), None, A.add), [("VD", 0, 8)], [("OFS", 8 * e, 8 * e + 8)])
+            op("v", ts(T.EQ[:, a:a + 128], T.VRO[:], T.VW[:, m:m + 1], 512.0, A.is_equal, A.mult),
+               [("VRO", 0, 128), ("VW", 0, 8)], [("EQ", a, a + 128)])
+        op("v", scan(T.LOS[:], T.EQ[:], T.KM[:], A.add, A.mult), [("EQ", 0, 1024), ("KM", 0, 1024)], [("LOS", 0, 1024)])
+        op("v", tt(T.VD[:], T.LOS[:, 127:1024:128], T.VW[:], A.add), [("LOS", 0, 1024), ("VW", 0, 8)], [("VD", 0, 8)])
+        op("v", cp(T.OFS[:], T.VD[:]), [("VD", 0, 8)], [("OFS", 0, 8)])
 
         for b in range(4):
             op("t", mm(T.psC[:, 512 * b:512 * b + 128], T.WQ[:, 128 * b:128 * b + 128], T.WSC[:, 128 * b:128 * b + 128],
@@ -367,12 +396,14 @@ def rank_program(g, core, T, topo):
             op("v", tt(T.TMP[:, a:a + 128], T.psC[:, 512 * b:512 * b + 128], T.OLD[:, a:a + 128], A.add),
                [("psC", 512 * b, 512 * b + 128), ("OLD", a, a + 128)], [("TMP", a, a + 128)])
             op("s", act(T.NV[:, a:a + 128], T.TMP[:, a:a + 128], ACT.Copy, scale=1.0 / 64), [("TMP", a, a + 128)], [("NV", a, a + 128)])
-        for b in range(2):
-            op("v", cp(T.X[:, 0:2560].indirect(T.OFS[:, 16 * b:16 * b + 16]), T.NV[:, 256 * b:256 * b + 256]),
-               [("OFS", 0, 32), ("NV", 256 * b, 256 * b + 256)], [("X", 0, 2560)])
+        for b in range(4):
+            op("v", cp(T["XP%d" % b][:, 0:1024].indirect(T.OFS[:, 0:8]), T.NV[:, 128 * b:128 * b + 128]),
+               [("OFS", 0, 8), ("NV", 128 * b, 128 * b + 128)], [("XP%d" % b, 0, 1024)])
 
-    op("v", lambda: V.quantize_mx(T.QX[:, 0:512], T.SX[:, 0:512], T.X[:, 0:2048]), [("X", 0, 2048)], [("QX", 0, 512), ("SX", 0, 512)])
-    nout = 2 * ROUNDS + 7
+    for e in range(4):
+        out, src = T.XF[:, e:2048:4], T["XP%d" % e][:, 0:512]
+        op("s" if e < 3 else "v", act(out, src, ACT.Copy) if e < 3 else cp(out, src), [("XP%d" % e, 0, 512)], [("XF.%d" % e, 0, 512)])
+    op("v", lambda: V.quantize_mx(T.QX[:, 0:512], T.SX[:, 0:512], T.XF[:, 0:2048]), [("XF.%d" % e, 0, 512) for e in range(4)], [("QX", 0, 512), ("SX", 0, 512)])
     for h in range(2):
         op("t", mm(T.psR[:, 1024 * h:1024 * h + 256], T.QWY[:, 0:128], T.SWY[:, 0:128], T.QX[:, 256 * h:256 * h + 256], T.SX[:, 256 * h:256 * h + 256]),
            [("QWY", 0, 128), ("SWY", 0, 128), ("QX", 0, 512), ("SX", 0, 512)], [("psR", 1024 * h, 1024 * h + 512)])

@@ -1,5 +1,4 @@
-from concourse.bass import DstId, RemoteDMATransfer
-from concourse.mybir import dt, AluOpType, AxisListType, ActivationFunctionType
+from concourse.mybir import dt, AluOpType, ActivationFunctionType
 
 ROUNDS = 3
 VCH = (2, 3, 4, 5, 6)
@@ -7,7 +6,7 @@ SCH = (0, 1, 7)
 
 F32, BF, F16, I32, U16, CODE, U8 = "float32", "bfloat16", "float16", "int32", "uint16", "float8_e4m3fn_x4", "uint8"
 SCRATCH = {
-    "XI": ("sbuf", [128, 2048], BF), "XF": ("sbuf", [128, 2048], BF), "H": ("sbuf", [128, 4096], BF),
+    "XI": ("sbuf", [128, 2048], BF), "XF": ("sbuf", [128, 4096], BF), "H": ("sbuf", [128, 4096], BF),
     "WQ": ("sbuf", [128, 512], CODE), "WSC": ("sbuf", [128, 512], U8),
     "UB": ("sbuf", [128, 512], BF), "QU": ("sbuf", [128, 128], CODE), "SU": ("sbuf", [128, 128], U8),
     "WYB": ("sbuf", [128, 512], BF), "QWY": ("sbuf", [128, 128], CODE), "SWY": ("sbuf", [128, 128], U8),
@@ -16,21 +15,23 @@ SCRATCH = {
     "FVP": ("sbuf", [128, 1024], I32), "POSL": ("sbuf", [128, 64], U16), "FVN": ("sbuf", [128, 1024], F32),
     "CC": ("sbuf", [128, 8], F32), "NCC": ("sbuf", [128, 4], F32),
     "EQR": ("sbuf", [128, 1024], BF), "SCB": ("sbuf", [128, 2880], F16), "JNK": ("sbuf", [128, 3480], BF),
-    "ASU": ("sbuf", [128, 4], F32), "APR": ("sbuf", [128, 4], F32), "RK": ("sbuf", [128, 8], F32),
-    "OFR": ("sbuf", [128, 8], U16), "WIN": ("sbuf", [128, 1024], F32), "T1": ("sbuf", [128, 128], F32),
-    "PK": ("sbuf", [128, 8], F32), "T2IN": ("sbuf", [128, 96], F32), "T2": ("sbuf", [128, 64], F32),
-    "BB": ("sbuf", [128, 256], F32), "BM": ("sbuf", [128, 256], F32),
-    "PW": ("sbuf", [128, 4], F32), "PI": ("sbuf", [128, 4], I32), "F8": ("sbuf", [128, 8], I32),
+    "ASU": ("sbuf", [128, 4], F32), "APR": ("sbuf", [128, 4], F32),
+    "OFR": ("sbuf", [128, 8], U16), "WIN": ("sbuf", [128, 1040], F32), "TT": ("sbuf", [128, 288], F32),
+    "SA": ("sbuf", [128, 16], F32), "SB": ("sbuf", [64, 16], F32), "SC": ("sbuf", [128, 16], F32),
+    "PP": ("sbuf", [128, 18], F32), "MK": ("sbuf", [128, 18], F32),
     "P32": ("sbuf", [128, 1], I32), "GI": ("sbuf", [128, 1], I32), "QI": ("sbuf", [128, 1], I32),
+    "HI": ("sbuf", [128, 1], I32), "HF": ("sbuf", [128, 1], F32), "NH": ("sbuf", [128, 1], F32),
     "GF": ("sbuf", [128, 1], F32), "QF": ("sbuf", [128, 1], F32), "Q64": ("sbuf", [128, 1], F32),
     "IV0": ("sbuf", [128, 128], F32), "IV": ("sbuf", [128, 128], F32),
     "MD0": ("sbuf", [128, 128], F32), "MD": ("sbuf", [128, 128], F32),
-    "KM0": ("sbuf", [128, 1024], F32), "KM": ("sbuf", [128, 1024], F16), "IOT": ("sbuf", [128, 1024], F32),
-    "RV0": ("sbuf", [128, 8], F32), "REV": ("sbuf", [128, 8], U16), "PL0": ("sbuf", [128, 64], F32),
+    "KM": ("sbuf", [128, 1024], F16), "IOT": ("sbuf", [128, 1024], F32),
+    "RV0": ("sbuf", [128, 8], F32), "QM": ("sbuf", [128, 8], F32), "REV": ("sbuf", [128, 8], U16),
+    "PL0": ("sbuf", [128, 128], F32),
     "VRO": ("sbuf", [128, 128], F16), "VM": ("sbuf", [128, 128], F32), "ZR": ("sbuf", [128, 128], F32),
     "VC": ("sbuf", [128, 144], F32), "VW": ("sbuf", [128, 8], F32), "EQ": ("sbuf", [128, 1024], F16),
     "LOS": ("sbuf", [128, 1024], F16), "VD": ("sbuf", [128, 8], F32),
-    "OFG": ("sbuf", [128, 8], U16), "OFS": ("sbuf", [128, 8], U16), "FR": ("sbuf", [128, 128], F32),
+    "OFG": ("sbuf", [128, 8], U16), "OFS": ("sbuf", [128, 8], U16), "OFX": ("sbuf", [128, 32], U16),
+    "FR": ("sbuf", [128, 128], F32),
     "OLD": ("sbuf", [128, 512], F32), "TMP": ("sbuf", [128, 512], F32), "NV": ("sbuf", [128, 512], BF),
     "YS": ("sbuf", [128, 512], F32),
     "psR": ("psum", [128, 2048], F32), "psC": ("psum", [128, 2048], F32),
@@ -64,7 +65,7 @@ def rank_program(g, core, T, topo):
     rank = T.rank_of(core)
     if rank is None:
         return
-    A, ACT, AX = AluOpType, ActivationFunctionType, AxisListType
+    A, ACT = AluOpType, ActivationFunctionType
     V, S, TE, SY = g.vector, g.scalar, g.tensor, g.sync
     queue = {"v": V, "s": S, "t": TE, "g": g, "y": SY}
     own = {"v": "cv", "s": "cs", "t": "ct", "g": "cg"}
@@ -138,11 +139,9 @@ def rank_program(g, core, T, topo):
     def mm(out, a, sa, b, sb):
         return lambda: TE.matmul_mx(out, a, sa, b, sb, True, True)
 
-    def iota(name, pattern, base, cm, n):
-        if SCRATCH[name][2] != I32:
-            op("g", lambda: g.iota(T[name][:], pattern, base, cm, allow_small_or_imprecise_dtypes=True), [], [(name, 0, n)])
-        else:
-            op("g", lambda: g.iota(T[name][:], pattern, base, cm), [], [(name, 0, n)])
+    def iota(name, pattern, base, cm, a, b):
+        kw = {} if SCRATCH[name][2] == I32 else {"allow_small_or_imprecise_dtypes": True}
+        op("g", lambda: g.iota(T[name][:, a:b], pattern, base, cm, **kw), [], [(name, a, b)])
 
     dma("y", T.XI[:], T.x[:], "dx", 1, [], [("XI", 0, 2048)])
     dma("s", T.FVT[:], T.fv[:], "dfv", 1, [], [("FVT", 0, 64)])
@@ -154,21 +153,35 @@ def rank_program(g, core, T, topo):
         dma("y", T.FVP[q:128:16, :], T.fv[:], "dfp", 16, [], [("FVP.%d" % q, 0, 1024)])
     dma("y", T.WYB[:], T.wy[:], "dwy", 1, [], [("WYB", 0, 512)])
 
-    iota("P32", [[0, 1]], 0, 1, 1)
-    iota("IV0", [[128, 8], [1, 16]], 0, 0, 128)
-    iota("MD0", [[0, 8], [1, 16]], 0, 0, 128)
-    iota("PL0", [[1, 64]], 0, 0, 64)
-    iota("RV0", [[-16, 8]], 127, 0, 8)
-    iota("KM0", [[-16, 8], [1, 128]], 0, 0, 1024)
-    iota("IOT", [[1, 1024]], 0, 0, 1024)
-    for e in range(4):
-        op("v", ts(T.OFH[:, 64 * e:64 * e + 64], T.FVT[:], 4.0, float(e), A.mult, A.add), [("FVT", 0, 64)], [("OFH", 64 * e, 64 * e + 64)])
-    op("v", cp(T.OFP[:], T.FVT[:]), [("FVT", 0, 64)], [("OFP", 0, 64)])
+    iota("P32", [[0, 1]], 0, 1, 0, 1)
+    iota("RV0", [[16, 8]], 0, 0, 0, 8)
+    iota("PL0", [[1, 128]], 0, 0, 0, 128)
+    iota("MD0", [[0, 8], [1, 16]], 0, 0, 0, 128)
+    col = 0
+    for first, n in ((VCH[0], len(VCH)), (SCH[0], 2), (SCH[2], 1)):
+        iota("IV0", [[128, n], [1, 16]], 128 * first, 0, col, col + 16 * n)
+        col += 16 * n
+    iota("IOT", [[1, 1024]], 0, 0, 0, 1024)
+    op("v", ms(T.WIN[:, 880:1040], 0.0), [], [("WIN", 880, 1040)])
+    op("v", ms(T.MK[:], 0.0), [], [("MK", 0, 18)])
+    op("v", ms(T.ZR[:], 0.0), [], [("ZR", 0, 128)])
+    op("v", ms(T.VC[:, 0:16], 0.0), [], [("VC", 0, 16)])
     op("v", ts(T.GI[:], T.P32[:], 4, None, A.arith_shift_right), [("P32", 0, 1)], [("GI", 0, 1)])
     op("v", ts(T.QI[:], T.P32[:], 15, None, A.bitwise_and), [("P32", 0, 1)], [("QI", 0, 1)])
-    op("v", ts(T.GF[:], T.GI[:], 16.0, None, A.mult), [("GI", 0, 1)], [("GF", 0, 1)])
+    op("v", ts(T.HI[:], T.GI[:], 1, None, A.bitwise_and), [("GI", 0, 1)], [("HI", 0, 1)])
     op("v", cp(T.QF[:], T.QI[:]), [("QI", 0, 1)], [("QF", 0, 1)])
+    op("v", ts(T.GF[:], T.GI[:], 16.0, None, A.mult), [("GI", 0, 1)], [("GF", 0, 1)])
+    op("v", cp(T.HF[:], T.HI[:]), [("HI", 0, 1)], [("HF", 0, 1)])
     op("v", ts(T.Q64[:], T.QI[:], 64.0, None, A.mult), [("QI", 0, 1)], [("Q64", 0, 1)])
+    op("v", ts(T.NH[:], T.HI[:], -1.0, 1.0, A.mult, A.add), [("HI", 0, 1)], [("NH", 0, 1)])
+    op("v", ts(T.QM[:], T.RV0[:], T.QF[:, 0:1], None, A.add), [("RV0", 0, 8), ("QF", 0, 1)], [("QM", 0, 8)])
+    for c in SCH:
+        op("v", ms(T["SG%d" % c][:, 6:7], float(128 * c - 896)), [], [("SG%d" % c, 6, 7)])
+        op("v", ts(T["SG%d" % c][:, 7:8], T.P32[:], -127.0, None, A.add), [("P32", 0, 1)], [("SG%d" % c, 7, 8)])
+    for a, s in ((0, "NH"), (4, "HF"), (9, "HF"), (14, "NH")):
+        op("v", ts(T.MK[:, a:a + 4], T.PL0[:, 0:4], 0.0, T[s][:, 0:1], A.mult, A.add), [("PL0", 0, 128), (s, 0, 1)], [("MK", a, a + 4)])
+    for e in range(4):
+        op("v", ts(T.OFH[:, 64 * e:64 * e + 64], T.FVT[:], 4.0, float(e), A.mult, A.add), [("FVT", 0, 64)], [("OFH", 64 * e, 64 * e + 64)])
     op("v", lambda: V.quantize_mx(T.QU[:, 0:128], T.SU[:, 0:128], T.UB[:, 0:512]), [("UB", 0, 512)], [("QU", 0, 128), ("SU", 0, 128)])
 
     def lay_u(t):
@@ -180,17 +193,13 @@ def rank_program(g, core, T, topo):
            [("SU", 0, 128), ("UO%d" % t, 0, 8)], [("SUR%d" % t, 0, 128)])
 
     lay_u(0)
-    op("v", ms(T.PK[:], 1.0), [], [("PK", 0, 8)])
-    for c in SCH:
-        op("v", ms(T["SG%d" % c][:, 6:7], float(128 * c - 896)), [], [("SG%d" % c, 6, 7)])
-        op("v", ts(T["SG%d" % c][:, 7:8], T.P32[:], -127.0, None, A.add), [("P32", 0, 1)], [("SG%d" % c, 7, 8)])
-    op("v", ms(T.T2IN[:], 0.0), [], [("T2IN", 0, 96)])
-    op("v", ms(T.PK[:, 0:8:4], 0.0), [], [("PK", 0, 8)])
-    op("v", ts(T.IV[:], T.IV0[:], T.GF[:, 0:1], None, A.add), [("IV0", 0, 128), ("GF", 0, 1)], [("IV", 0, 128)])
-    op("v", ms(T.PK[:, 2:8:4], 1024.0), [], [("PK", 0, 8)])
+    op("v", cp(T.OFP[:], T.FVT[:]), [("FVT", 0, 64)], [("OFP", 0, 64)])
+    op("v", ts(T.POSL[:], T.PL0[:, 0:64], T.Q64[:, 0:1], None, A.add), [("PL0", 0, 128), ("Q64", 0, 1)], [("POSL", 0, 64)])
     op("v", ts(T.MD[:], T.MD0[:], T.QF[:, 0:1], None, A.is_equal), [("MD0", 0, 128), ("QF", 0, 1)], [("MD", 0, 128)])
-    op("v", ts(T.POSL[:], T.PL0[:], T.Q64[:, 0:1], None, A.add), [("PL0", 0, 64), ("Q64", 0, 1)], [("POSL", 0, 64)])
-    op("v", ts(T.REV[:], T.RV0[:], T.QF[:, 0:1], None, A.subtract), [("RV0", 0, 8), ("QF", 0, 1)], [("REV", 0, 8)])
+    op("v", ts(T.IV[:], T.IV0[:], T.GF[:, 0:1], None, A.add), [("IV0", 0, 128), ("GF", 0, 1)], [("IV", 0, 128)])
+    op("v", ts(T.REV[:], T.QM[:], -1.0, 127.0, A.mult, A.add), [("QM", 0, 8)], [("REV", 0, 8)])
+    for m in range(8):
+        op("v", ts(T.KM[:, 128 * m:128 * m + 128], T.PL0[:], T.QM[:, m:m + 1], None, A.is_gt), [("PL0", 0, 128), ("QM", 0, 8)], [("KM", 128 * m, 128 * m + 128)])
 
     partners = [T.cores[rank ^ (1 << t)] for t in range(ROUNDS)]
     common = [e for e in topo.engines(core, partners[0]) if all(e in topo.engines(core, p) for p in partners)]
@@ -306,6 +315,9 @@ def rank_program(g, core, T, topo):
                [(nm, 6, d)], [("APR", i, i + 1), ("JNK", j + 6, j + d)])
             op("s", act(T.JNK[:, j + d:j + 1160], sg[:, d:1160], ACT.Relu, accum_out=T.ASU[:, i:i + 1]),
                [(nm, d, 1160)], [("ASU", i, i + 1), ("JNK", j + d, j + 1160)])
+        if t == 0:
+            op("s", act(T.FVN[:], T.FVP[:].indirect(T.POSL[:, 0:64]), ACT.Copy),
+               [("FVP.%d" % q, 0, 1024) for q in range(16)] + [("POSL", 0, 64)], [("FVN", 0, 1024)])
         beat(2, 512, 1024, A.is_le)
         eq(4)
         beat(3, 512, 1024, A.is_le)
@@ -318,64 +330,54 @@ def rank_program(g, core, T, topo):
             beat(c, 128 * c + 128, 1024, A.is_le)
             total_of(i - 1)
         total_of(4)
-        op("v", cp(T.RK[:, 2:7], T.SCB[:, 575:2880:576]), [("SCB", 0, 2880)], [("RK", 2, 7)])
-        op("v", tt(T.RK[:, 0:2], T.APR[:, 0:2], T.ASU[:, 0:2], A.subtract), [("ASU", 0, 2), ("APR", 0, 2)], [("RK", 0, 2)])
-        op("v", tt(T.RK[:, 7:8], T.APR[:, 2:3], T.ASU[:, 2:3], A.subtract), [("ASU", 2, 3), ("APR", 2, 3)], [("RK", 7, 8)])
-        op("v", cp(T.OFR[:], T.RK[:]), [("RK", 0, 8)], [("OFR", 0, 8)])
+        op("v", cp(T.OFR[:, 0:5], T.SCB[:, 575:2880:576]), [("SCB", 0, 2880)], [("OFR", 0, 5)])
+        op("v", tt(T.OFR[:, 5:8], T.APR[:, 0:3], T.ASU[:, 0:3], A.subtract), [("ASU", 0, 3), ("APR", 0, 3)], [("OFR", 5, 8)])
         op("v", cp(T.WIN[:, 0:1024].indirect(T.OFR[:, 0:8]), T.IV[:]), [("OFR", 0, 8), ("IV", 0, 128)], [("WIN", 0, 1024)])
-        op("v", lambda: V.transpose(T.T1[:], T.WIN[:, 896:1024]), [("WIN", 896, 1024)], [("T1", 0, 128)])
-        op("v", scan(T.T2IN[:, 8:65:8], T.PK[:], T.T1[:, 0:128:16], A.mult, A.add), [("T1", 0, 128), ("PK", 0, 8)], [("T2IN", 0, 96)])
-        op("v", lambda: V.transpose(T.T2[:], T.T2IN[:, 32:96]), [("T2IN", 0, 96)], [("T2", 0, 64)])
-        for a in range(4):
-            op("g", lambda: g.partition_broadcast(T.BB[:, 64 * a:64 * a + 64], T.T2[32 * a:32 * a + 1, 0:64], 128),
-               [("T2", 0, 64)], [("BB", 64 * a, 64 * a + 64)])
-        if t == 0:
-            op("v", cp(T.FVN[:], T.FVP[:].indirect(T.POSL[:, 0:64])),
-               [("FVP.%d" % q, 0, 1024) for q in range(16)] + [("POSL", 0, 64)], [("FVN", 0, 1024)])
-        for a in range(4):
-            op("v", tt(T.BM[:, a:256:4], T.BB[:, 64 * a:64 * a + 64], T.MD[:, 0:64], A.mult),
-               [("BB", 64 * a, 64 * a + 64), ("MD", 0, 128)], [("BM.%d" % a, 0, 256)])
-        for m in range(4):
-            op("v", lambda: V.tensor_reduce(T.PW[:, m:m + 1], T.BM[:, 64 * m:64 * m + 64], AX.X, A.add),
-               [("BM.%d" % a, 0, 256) for a in range(4)], [("PW", m, m + 1)])
-        op("v", cp(T.PI[:], T.PW[:]), [("PW", 0, 4)], [("PI", 0, 4)])
-        for b in range(2):
-            op("v", ts(T.F8[:, 4 * b:4 * b + 2], T.PI[:, 2 * b:2 * b + 2], 10, None, A.arith_shift_right), [("PI", 0, 4)], [("F8", 4 * b, 4 * b + 2)])
-            op("v", ts(T.F8[:, 4 * b + 2:4 * b + 4], T.PI[:, 2 * b:2 * b + 2], 1023, None, A.bitwise_and), [("PI", 0, 4)], [("F8", 4 * b + 2, 4 * b + 4)])
+        op("v", lambda: V.transpose(T.TT[:, 0:128], T.WIN[:, 896:1024]), [("WIN", 896, 1024)], [("TT.0", 0, 128)])
+        op("v", lambda: V.transpose(T.TT[:, 128:288], T.WIN[:, 880:1040]), [("WIN", 880, 1040)], [("TT.1", 0, 160)])
+        op("v", tt(T.SA[:, 0:9], T.TT[:, 0:288:32], T.TT[:, 16:288:32], A.add), [("TT.0", 0, 128), ("TT.1", 0, 160)], [("SA", 0, 9)])
+        op("v", tt(T.SB[0:64, 0:9], T.SA[0:64, 0:9], T.SA[64:128, 0:9], A.add), [("SA", 0, 9)], [("SB", 0, 9)])
+        op("v", tt(T.SC[0:32, 0:9], T.SB[0:32, 0:9], T.SB[32:64, 0:9], A.add), [("SB", 0, 9)], [("SC", 0, 9)])
+        op("v", cp(T.SC[32:64, 0:9], T.SC[0:32, 0:9]), [("SC", 0, 9)], [("SC", 0, 9)])
+        op("v", cp(T.SC[64:128, 0:9], T.SC[0:64, 0:9]), [("SC", 0, 9)], [("SC", 0, 9)])
         LST, nL = T["LST%d" % t], "LST%d" % t
-        op("v", cp(LST[:], T.F8[:]), [("F8", 0, 8)], [(nL, 0, 8)])
+        op("v", tt(T.PP[:, 0:9], T.SC[:, 0:9], T.MK[:, 0:9], A.mult), [("SC", 0, 9), ("MK", 0, 18)], [("PP", 0, 9)])
+        op("v", tt(T.PP[:, 9:18], T.SC[:, 0:9], T.MK[:, 9:18], A.mult), [("SC", 0, 9), ("MK", 0, 18)], [("PP", 9, 18)])
+        op("v", tt(LST[:, 0:8:2], T.PP[:, 0:4], T.PP[:, 4:8], A.add), [("PP", 0, 9)], [(nL + ".0", 0, 8)])
+        op("v", tt(LST[:, 1:8:2], T.PP[:, 9:13], T.PP[:, 14:18], A.add), [("PP", 9, 18)], [(nL + ".1", 0, 8)])
+        rL = [(nL + ".0", 0, 8), (nL + ".1", 0, 8)]
 
-        send(t, T["LR%d" % t][:], LST[:], "arrL%d" % t, [(nL, 0, 8)])
+        send(t, T["LR%d" % t][:], LST[:], "arrL%d" % t, rL)
         op("v", cp(T["SL%d" % t][:, 0:128].bitcast(dt.uint32), QH[:, 0:1024].bitcast(dt.uint32).indirect(LST[:, 0:8])),
-           [(nQH, 0, 1024), (nL, 0, 8)], [("SL%d" % t, 0, 128)])
+           [(nQH, 0, 1024)] + rL, [("SL%d" % t, 0, 128)])
         op("s", act(T["SS%d" % t][:, 0:128], SH[:, 0:1024].indirect(LST[:, 0:8]), ACT.Copy),
-           [(nSH, 0, 1024), (nL, 0, 8)], [("SS%d" % t, 0, 128)])
+           [(nSH, 0, 1024)] + rL, [("SS%d" % t, 0, 128)])
         send(t, T["LC%d" % t][:, 0:128].bitcast(dt.uint8), T["SL%d" % t][:, 0:128].bitcast(dt.uint8), "arrC%d" % t, [("SL%d" % t, 0, 128)])
         send(t, T["LS%d" % t][:, 0:128], T["SS%d" % t][:, 0:128], "arrS%d" % t, [("SS%d" % t, 0, 128)])
         note("a", ("arrL%d" % t, ne), [], [("LR%d" % t, 0, 8)])
         note("a", ("arrC%d" % t, ne), [], [("LC%d" % t, 0, 128)])
         note("a", ("arrS%d" % t, ne), [], [("LS%d" % t, 0, 128)])
         FLS, nF = T["FLS%d" % t], "FLS%d" % t
-        op("s", act(T.FR[:], T.IOT[:].indirect(LST[:, 0:8]), ACT.Copy), [("IOT", 0, 1024), (nL, 0, 8)], [("FR", 0, 128)])
+        op("s", act(T.FR[:], T.IOT[:].indirect(LST[:, 0:8]), ACT.Copy), [("IOT", 0, 1024)] + rL, [("FR", 0, 128)])
         op("s", act(FLS[:], T.FR[:].indirect(T.REV[:, 0:8]), ACT.Copy), [("FR", 0, 128), ("REV", 0, 8)], [(nF, 0, 128)])
         dma("y", T.fl[t:t + 1, :], FLS[0:1, :], "dout", nout, [(nF, 0, 128)], [])
         if t == 0:
-            op("v", ms(T.ZR[:], 0.0), [], [("ZR", 0, 128)])
-            op("v", ms(T.VC[:, 0:16], 0.0), [], [("VC", 0, 16)])
-            op("v", ts(T.KM[:], T.KM0[:], T.QF[:, 0:1], None, A.is_gt), [("KM0", 0, 1024), ("QF", 0, 1)], [("KM", 0, 1024)])
-            lay_u(1)
             for e in range(4):
-                op("s", act(T["XP%d" % e][:, 0:512], T.XI[:, e:2048:4], ACT.Copy), [("XI", 0, 2048)], [("XP%d" % e, 0, 512)])
+                op("v", cp(T["XP%d" % e][:, 0:512], T.XI[:, e:2048:4]), [("XI", 0, 2048)], [("XP%d" % e, 0, 512)])
+            lay_u(1)
         if t == 1:
             lay_u(2)
             op("v", lambda: V.quantize_mx(T.QWY[:, 0:128], T.SWY[:, 0:128], T.WYB[:, 0:512]), [("WYB", 0, 512)], [("QWY", 0, 128), ("SWY", 0, 128)])
+        if t == 2:
+            for e in range(4):
+                op("v", cp(T.XF[:, e:2048:4], T["XP%d" % e][:, 0:512]), [("XP%d" % e, 0, 512)], [("XF.%d" % e, 0, 4096)])
 
         LR, nR = T["LR%d" % t], "LR%d" % t
         op("v", tt(T.VM[:], T.FVN[:].indirect(LR[:, 0:8]), T.MD[:], A.mult), [("FVN", 0, 1024), (nR, 0, 8), ("MD", 0, 128)], [("VM", 0, 128)])
-        op("v", cp(T.VRO[:], T.FVN[:].indirect(LR[:, 0:8])), [("FVN", 0, 1024), (nR, 0, 8)], [("VRO", 0, 128)])
+        op("s", act(T.VRO[:], T.FVN[:].indirect(LR[:, 0:8]), ACT.Copy), [("FVN", 0, 1024), (nR, 0, 8)], [("VRO", 0, 128)])
         op("v", scan(T.VC[:, 16:144], T.VM[:], T.ZR[:], A.add, A.add), [("VM", 0, 128), ("ZR", 0, 128)], [("VC", 16, 144)])
+        op("v", tt(T.OFG[:], T.VC[:, 31:144:16], T.VC[:, 15:128:16], A.subtract), [("VC", 0, 144)], [("OFG", 0, 8)])
         op("v", tt(T.VW[:], T.VC[:, 31:144:16], T.VC[:, 15:128:16], A.subtract), [("VC", 0, 144)], [("VW", 0, 8)])
-        op("v", cp(T.OFG[:], T.VW[:]), [("VW", 0, 8)], [("OFG", 0, 8)])
         for e in range(4):
             op("s", act(T.OLD[:, 128 * e:128 * e + 128], T["XP%d" % e][:, 0:512].indirect(T.OFG[:, 0:8]), ACT.Copy, scale=32.0),
                [("XP%d" % e, 0, 512), ("OFG", 0, 8)], [("OLD", 128 * e, 128 * e + 128)])
@@ -384,8 +386,12 @@ def rank_program(g, core, T, topo):
             op("v", ts(T.EQ[:, a:a + 128], T.VRO[:], T.VW[:, m:m + 1], 512.0, A.is_equal, A.mult),
                [("VRO", 0, 128), ("VW", 0, 8)], [("EQ", a, a + 128)])
         op("v", scan(T.LOS[:], T.EQ[:], T.KM[:], A.add, A.mult), [("EQ", 0, 1024), ("KM", 0, 1024)], [("LOS", 0, 1024)])
-        op("v", tt(T.VD[:], T.LOS[:, 127:1024:128], T.VW[:], A.add), [("LOS", 0, 1024), ("VW", 0, 8)], [("VD", 0, 8)])
-        op("v", cp(T.OFS[:], T.VD[:]), [("VD", 0, 8)], [("OFS", 0, 8)])
+        if t < 2:
+            op("v", tt(T.OFS[:], T.LOS[:, 127:1024:128], T.VW[:], A.add), [("LOS", 0, 1024), ("VW", 0, 8)], [("OFS", 0, 8)])
+        else:
+            op("v", tt(T.VD[:], T.LOS[:, 127:1024:128], T.VW[:], A.add), [("LOS", 0, 1024), ("VW", 0, 8)], [("VD", 0, 8)])
+            for e in range(4):
+                op("v", ts(T.OFX[:, 8 * e:8 * e + 8], T.VD[:], 4.0, float(e), A.mult, A.add), [("VD", 0, 8)], [("OFX", 8 * e, 8 * e + 8)])
 
         for b in range(4):
             op("t", mm(T.psC[:, 512 * b:512 * b + 128], T.WQ[:, 128 * b:128 * b + 128], T.WSC[:, 128 * b:128 * b + 128],
@@ -397,23 +403,26 @@ def rank_program(g, core, T, topo):
                [("psC", 512 * b, 512 * b + 128), ("OLD", a, a + 128)], [("TMP", a, a + 128)])
             op("s", act(T.NV[:, a:a + 128], T.TMP[:, a:a + 128], ACT.Copy, scale=1.0 / 64), [("TMP", a, a + 128)], [("NV", a, a + 128)])
         for b in range(4):
-            op("v", cp(T["XP%d" % b][:, 0:1024].indirect(T.OFS[:, 0:8]), T.NV[:, 128 * b:128 * b + 128]),
-               [("OFS", 0, 8), ("NV", 128 * b, 128 * b + 128)], [("XP%d" % b, 0, 1024)])
+            if t < 2:
+                op("v", cp(T["XP%d" % b][:, 0:1024].indirect(T.OFS[:, 0:8]), T.NV[:, 128 * b:128 * b + 128]),
+                   [("OFS", 0, 8), ("NV", 128 * b, 128 * b + 128)], [("XP%d" % b, 0, 1024)])
+            else:
+                op("v", cp(T.XF[:, 0:4096].indirect(T.OFX[:, 8 * b:8 * b + 8]), T.NV[:, 128 * b:128 * b + 128]),
+                   [("OFX", 0, 32), ("NV", 128 * b, 128 * b + 128)], [("XF.%d" % e, 0, 4096) for e in range(4)])
 
-    for e in range(4):
-        out, src = T.XF[:, e:2048:4], T["XP%d" % e][:, 0:512]
-        op("s" if e < 3 else "v", act(out, src, ACT.Copy) if e < 3 else cp(out, src), [("XP%d" % e, 0, 512)], [("XF.%d" % e, 0, 512)])
-    op("v", lambda: V.quantize_mx(T.QX[:, 0:512], T.SX[:, 0:512], T.XF[:, 0:2048]), [("XF.%d" % e, 0, 512) for e in range(4)], [("QX", 0, 512), ("SX", 0, 512)])
     for h in range(2):
-        op("t", mm(T.psR[:, 1024 * h:1024 * h + 256], T.QWY[:, 0:128], T.SWY[:, 0:128], T.QX[:, 256 * h:256 * h + 256], T.SX[:, 256 * h:256 * h + 256]),
-           [("QWY", 0, 128), ("SWY", 0, 128), ("QX", 0, 512), ("SX", 0, 512)], [("psR", 1024 * h, 1024 * h + 512)])
+        a = 256 * h
+        op("v", lambda: V.quantize_mx(T.QX[:, a:a + 256], T.SX[:, a:a + 256], T.XF[:, 4 * a:4 * a + 1024]),
+           [("XF.%d" % e, 0, 4096) for e in range(4)], [("QX", a, a + 256), ("SX", a, a + 256)])
+        op("t", mm(T.psR[:, 1024 * h:1024 * h + 256], T.QWY[:, 0:128], T.SWY[:, 0:128], T.QX[:, a:a + 256], T.SX[:, a:a + 256]),
+           [("QWY", 0, 128), ("SWY", 0, 128), ("QX", a, a + 256), ("SX", a, a + 256)], [("psR", 1024 * h, 1024 * h + 512)])
+    op("s", act(T.YS[:, 0:256], T.psR[:, 0:256], ACT.Copy), [("psR", 0, 256)], [("YS", 0, 256)])
+    op("v", cp(T.YS[:, 256:512], T.psR[:, 1024:1280]), [("psR", 1024, 1280)], [("YS", 256, 512)])
     dma("y", T.oc[:, 0:2048], T.QX[:, 0:512].bitcast(dt.uint8), "dout", nout, [("QX", 0, 512)], [])
-    op("v", cp(T.YS[:, 0:256], T.psR[:, 0:256]), [("psR", 0, 256)], [("YS", 0, 256)])
-    op("s", act(T.YS[:, 256:512], T.psR[:, 1024:1280], ACT.Copy), [("psR", 1024, 1280)], [("YS", 256, 512)])
-    dma("s", T.y[:, 256:512], T.YS[:, 256:512], "dout", nout, [("YS", 256, 512)], [])
-    dma("y", T.y[:, 0:256], T.YS[:, 0:256], "dout", nout, [("YS", 0, 256)], [])
+    dma("s", T.y[:, 0:256], T.YS[:, 0:256], "dout", nout, [("YS", 0, 256)], [])
+    dma("y", T.y[:, 256:512], T.YS[:, 256:512], "dout", nout, [("YS", 256, 512)], [])
     for k in range(4):
-        dma("s" if k % 2 else "y", T.osc[4 * k:4 * k + 4, :], T.SX[32 * k:32 * k + 4, 0:512], "dout", nout, [("SX", 0, 512)], [])
+        dma("y" if k % 2 else "s", T.osc[4 * k:4 * k + 4, :], T.SX[32 * k:32 * k + 4, 0:512], "dout", nout, [("SX", 0, 512)], [])
     for sem in sorted(total):
         if most.get(sem, 0) < total[sem]:
             need("g", (sem, total[sem]))

from concourse.mybir import dt, AluOpType, ActivationFunctionType

ROUNDS = 3
VCH = (2, 3, 4, 5, 6)
SCH = (0, 1, 7)

F32, BF, F16, I32, U16, CODE, U8 = "float32", "bfloat16", "float16", "int32", "uint16", "float8_e4m3fn_x4", "uint8"
SCRATCH = {
    "XI": ("sbuf", [128, 2048], BF), "XF": ("sbuf", [128, 4096], BF), "H": ("sbuf", [128, 4096], BF),
    "WQ": ("sbuf", [128, 512], CODE), "WSC": ("sbuf", [128, 512], U8),
    "UB": ("sbuf", [128, 512], BF), "QU": ("sbuf", [128, 128], CODE), "SU": ("sbuf", [128, 128], U8),
    "WYB": ("sbuf", [128, 512], BF), "QWY": ("sbuf", [128, 128], CODE), "SWY": ("sbuf", [128, 128], U8),
    "QX": ("sbuf", [128, 512], CODE), "SX": ("sbuf", [128, 512], U8),
    "FVT": ("sbuf", [128, 64], I32), "OFH": ("sbuf", [128, 256], U16), "OFP": ("sbuf", [128, 64], U16),
    "FVP": ("sbuf", [128, 1024], I32), "POSL": ("sbuf", [128, 64], U16), "FVN": ("sbuf", [128, 1024], F32),
    "CC": ("sbuf", [128, 8], F32), "NCC": ("sbuf", [128, 4], F32),
    "EQR": ("sbuf", [128, 1024], BF), "SCB": ("sbuf", [128, 2880], F16), "JNK": ("sbuf", [128, 3480], BF),
    "ASU": ("sbuf", [128, 4], F32), "APR": ("sbuf", [128, 4], F32),
    "OFR": ("sbuf", [128, 8], U16), "WIN": ("sbuf", [128, 1040], F32), "TT": ("sbuf", [128, 288], F32),
    "SA": ("sbuf", [128, 16], F32), "SB": ("sbuf", [64, 16], F32), "SC": ("sbuf", [128, 16], F32),
    "PP": ("sbuf", [128, 18], F32), "MK": ("sbuf", [128, 18], F32),
    "P32": ("sbuf", [128, 1], I32), "GI": ("sbuf", [128, 1], I32), "QI": ("sbuf", [128, 1], I32),
    "HI": ("sbuf", [128, 1], I32), "HF": ("sbuf", [128, 1], F32), "NH": ("sbuf", [128, 1], F32),
    "GF": ("sbuf", [128, 1], F32), "QF": ("sbuf", [128, 1], F32), "Q64": ("sbuf", [128, 1], F32),
    "IV0": ("sbuf", [128, 128], F32), "IV": ("sbuf", [128, 128], F32),
    "MD0": ("sbuf", [128, 128], F32), "MD": ("sbuf", [128, 128], F32),
    "KM": ("sbuf", [128, 1024], F16), "IOT": ("sbuf", [128, 1024], F32),
    "RV0": ("sbuf", [128, 8], F32), "QM": ("sbuf", [128, 8], F32), "REV": ("sbuf", [128, 8], U16),
    "PL0": ("sbuf", [128, 128], F32),
    "VRO": ("sbuf", [128, 128], F16), "VM": ("sbuf", [128, 128], F32), "ZR": ("sbuf", [128, 128], F32),
    "VC": ("sbuf", [128, 144], F32), "VW": ("sbuf", [128, 8], F32), "EQ": ("sbuf", [128, 1024], F16),
    "LOS": ("sbuf", [128, 1024], F16), "VD": ("sbuf", [128, 8], F32),
    "OFG": ("sbuf", [128, 8], U16), "OFS": ("sbuf", [128, 8], U16), "OFX": ("sbuf", [128, 32], U16),
    "FR": ("sbuf", [128, 128], F32),
    "OLD": ("sbuf", [128, 512], F32), "TMP": ("sbuf", [128, 512], F32), "NV": ("sbuf", [128, 512], BF),
    "YS": ("sbuf", [128, 512], F32),
    "psR": ("psum", [128, 2048], F32), "psC": ("psum", [128, 2048], F32),
}
for _e in range(4):
    SCRATCH["XP%d" % _e] = ("sbuf", [128, 1024], BF)
for _c in VCH:
    SCRATCH["CB%d" % _c] = ("sbuf", [128, 1152], BF)
for _c in SCH:
    SCRATCH["SG%d" % _c] = ("sbuf", [128, 1160], BF)
for _t in range(ROUNDS):
    SCRATCH["UO%d" % _t] = ("sbuf", [128, 8], U16)
    SCRATCH["QUR%d" % _t] = ("sbuf", [128, 128], CODE)
    SCRATCH["SUR%d" % _t] = ("sbuf", [128, 128], U8)
    SCRATCH["QH%d" % _t] = ("sbuf", [128, 1024], CODE)
    SCRATCH["SH%d" % _t] = ("sbuf", [128, 1024], U8)
    SCRATCH["SL%d" % _t] = ("sbuf", [128, 128], CODE)
    SCRATCH["SS%d" % _t] = ("sbuf", [128, 128], U8)
    SCRATCH["LC%d" % _t] = ("sbuf", [128, 128], CODE)
    SCRATCH["LS%d" % _t] = ("sbuf", [128, 128], U8)
    SCRATCH["LR%d" % _t] = ("sbuf", [128, 8], U16)
    SCRATCH["LST%d" % _t] = ("sbuf", [128, 8], U16)
    SCRATCH["FLS%d" % _t] = ("sbuf", [128, 128], F32)

SEMAPHORES = ["cv", "cs", "ct", "cg", "dx", "dfv", "du", "dfp", "dw", "dwy", "dout", "sent"]
for _t in range(ROUNDS):
    SEMAPHORES += ["arrL%d" % _t, "arrC%d" % _t, "arrS%d" % _t]


def rank_program(g, core, T, topo):
    rank = T.rank_of(core)
    if rank is None:
        return
    A, ACT = AluOpType, ActivationFunctionType
    V, S, TE, SY = g.vector, g.scalar, g.tensor, g.sync
    queue = {"v": V, "s": S, "t": TE, "g": g, "y": SY}
    own = {"v": "cv", "s": "cs", "t": "ct", "g": "cg"}

    count = {k: 0 for k in own}
    known = {k: {} for k in queue}
    most, total = {}, {}
    wr, rd = {}, {}

    def need(e, tok):
        sem, n = tok
        if known[e].get(sem, 0) < n:
            queue[e].wait_ge(T.sem[sem], n)
            known[e][sem] = n
            most[sem] = max(most.get(sem, 0), n)

    def deps(e, reads, writes):
        want = {}
        for n, a, b in reads:
            for (x, y, tok, w) in wr.get(n, []):
                if x < b and a < y:
                    want[tok[0]] = max(want.get(tok[0], 0), tok[1])
        for n, a, b in writes:
            for (x, y, tok, w) in wr.get(n, []):
                if x < b and a < y:
                    want[tok[0]] = max(want.get(tok[0], 0), tok[1])
            for (x, y, tok, w) in rd.get(n, []):
                if x < b and a < y and w != e:
                    want[tok[0]] = max(want.get(tok[0], 0), tok[1])
        for sem in sorted(want):
            need(e, (sem, want[sem]))

    def note(e, tok, reads, writes):
        for n, a, b in writes:
            wr[n] = [r for r in wr.get(n, []) if not (a <= r[0] and r[1] <= b)] + [(a, b, tok, e)]
            rd[n] = [r for r in rd.get(n, []) if not (a <= r[0] and r[1] <= b)]
        for n, a, b in reads:
            rd[n] = [r for r in rd.get(n, []) if not (r[3] == e and a <= r[0] and r[1] <= b)] + [(a, b, tok, e)]

    def op(e, call, reads, writes):
        deps(e, reads, writes)
        count[e] += 1
        total[own[e]] = count[e]
        call().then_inc(T.sem[own[e]], 1)
        note(e, (own[e], count[e]), reads, writes)

    def dma(e, out, in_, sem, n, reads, writes):
        deps(e, reads, writes)
        total[sem] = total.get(sem, 0) + 16
        queue[e].dma_start(out, in_).then_inc(T.sem[sem], 16)
        note("d" + sem, (sem, 16 * n), reads, writes)

    def ts(out, in0, s1, s2, *ops):
        return lambda: V.tensor_scalar(out, in0, s1, s2, *ops)

    def tt(out, a, b, o):
        return lambda: V.tensor_tensor(out, a, b, o)

    def scan(out, a, b, o0, o1):
        return lambda: V.tensor_tensor_scan(out, a, b, 0.0, o0, o1)

    def cp(out, in_):
        return lambda: V.tensor_copy(out, in_)

    def ms(ap, c):
        return lambda: V.memset(ap, c)

    def act(out, in_, func, **kw):
        return lambda: S.activation(out, in_, func, **kw)

    def mm(out, a, sa, b, sb):
        return lambda: TE.matmul_mx(out, a, sa, b, sb, True, True)

    def iota(name, pattern, base, cm, a, b):
        kw = {} if SCRATCH[name][2] == I32 else {"allow_small_or_imprecise_dtypes": True}
        op("g", lambda: g.iota(T[name][:, a:b], pattern, base, cm, **kw), [], [(name, a, b)])

    dma("y", T.XI[:], T.x[:], "dx", 1, [], [("XI", 0, 2048)])
    dma("s", T.FVT[:], T.fv[:], "dfv", 1, [], [("FVT", 0, 64)])
    dma("s", T.UB[:], T.u[:], "du", 1, [], [("UB", 0, 512)])
    need("y", ("dx", 16))
    dma("y", T.WQ[:, 0:512].bitcast(dt.uint8), T.wc[:], "dw", 2, [], [("WQ", 0, 512)])
    dma("y", T.WSC[:, 0:512], T.ws[:], "dw", 2, [], [("WSC", 0, 512)])
    for q in range(16):
        dma("y", T.FVP[q:128:16, :], T.fv[:], "dfp", 16, [], [("FVP.%d" % q, 0, 1024)])
    dma("y", T.WYB[:], T.wy[:], "dwy", 1, [], [("WYB", 0, 512)])

    iota("P32", [[0, 1]], 0, 1, 0, 1)
    iota("RV0", [[16, 8]], 0, 0, 0, 8)
    iota("PL0", [[1, 128]], 0, 0, 0, 128)
    iota("MD0", [[0, 8], [1, 16]], 0, 0, 0, 128)
    col = 0
    for first, n in ((VCH[0], len(VCH)), (SCH[0], 2), (SCH[2], 1)):
        iota("IV0", [[128, n], [1, 16]], 128 * first, 0, col, col + 16 * n)
        col += 16 * n
    iota("IOT", [[1, 1024]], 0, 0, 0, 1024)
    op("v", ms(T.WIN[:, 880:1040], 0.0), [], [("WIN", 880, 1040)])
    op("v", ms(T.MK[:], 0.0), [], [("MK", 0, 18)])
    op("v", ms(T.ZR[:], 0.0), [], [("ZR", 0, 128)])
    op("v", ms(T.VC[:, 0:16], 0.0), [], [("VC", 0, 16)])
    op("v", ts(T.GI[:], T.P32[:], 4, None, A.arith_shift_right), [("P32", 0, 1)], [("GI", 0, 1)])
    op("v", ts(T.QI[:], T.P32[:], 15, None, A.bitwise_and), [("P32", 0, 1)], [("QI", 0, 1)])
    op("v", ts(T.HI[:], T.GI[:], 1, None, A.bitwise_and), [("GI", 0, 1)], [("HI", 0, 1)])
    op("v", cp(T.QF[:], T.QI[:]), [("QI", 0, 1)], [("QF", 0, 1)])
    op("v", ts(T.GF[:], T.GI[:], 16.0, None, A.mult), [("GI", 0, 1)], [("GF", 0, 1)])
    op("v", cp(T.HF[:], T.HI[:]), [("HI", 0, 1)], [("HF", 0, 1)])
    op("v", ts(T.Q64[:], T.QI[:], 64.0, None, A.mult), [("QI", 0, 1)], [("Q64", 0, 1)])
    op("v", ts(T.NH[:], T.HI[:], -1.0, 1.0, A.mult, A.add), [("HI", 0, 1)], [("NH", 0, 1)])
    op("v", ts(T.QM[:], T.RV0[:], T.QF[:, 0:1], None, A.add), [("RV0", 0, 8), ("QF", 0, 1)], [("QM", 0, 8)])
    for c in SCH:
        op("v", ms(T["SG%d" % c][:, 6:7], float(128 * c - 896)), [], [("SG%d" % c, 6, 7)])
        op("v", ts(T["SG%d" % c][:, 7:8], T.P32[:], -127.0, None, A.add), [("P32", 0, 1)], [("SG%d" % c, 7, 8)])
    for a, s in ((0, "NH"), (4, "HF"), (9, "HF"), (14, "NH")):
        op("v", ts(T.MK[:, a:a + 4], T.PL0[:, 0:4], 0.0, T[s][:, 0:1], A.mult, A.add), [("PL0", 0, 128), (s, 0, 1)], [("MK", a, a + 4)])
    for e in range(4):
        op("v", ts(T.OFH[:, 64 * e:64 * e + 64], T.FVT[:], 4.0, float(e), A.mult, A.add), [("FVT", 0, 64)], [("OFH", 64 * e, 64 * e + 64)])
    op("v", lambda: V.quantize_mx(T.QU[:, 0:128], T.SU[:, 0:128], T.UB[:, 0:512]), [("UB", 0, 512)], [("QU", 0, 128), ("SU", 0, 128)])

    def lay_u(t):
        op("v", ms(T["UO%d" % t][:], t), [], [("UO%d" % t, 0, 8)])
        off = T["UO%d" % t]
        op("v", cp(T["QUR%d" % t][:, 0:128].bitcast(dt.uint32), T.QU[:, 0:128].bitcast(dt.uint32).indirect(off[:, 0:8])),
           [("QU", 0, 128), ("UO%d" % t, 0, 8)], [("QUR%d" % t, 0, 128)])
        op("v", cp(T["SUR%d" % t][:, 0:128], T.SU[:, 0:128].indirect(off[:, 0:8])),
           [("SU", 0, 128), ("UO%d" % t, 0, 8)], [("SUR%d" % t, 0, 128)])

    lay_u(0)
    op("v", cp(T.OFP[:], T.FVT[:]), [("FVT", 0, 64)], [("OFP", 0, 64)])
    op("v", ts(T.POSL[:], T.PL0[:, 0:64], T.Q64[:, 0:1], None, A.add), [("PL0", 0, 128), ("Q64", 0, 1)], [("POSL", 0, 64)])
    op("v", ts(T.MD[:], T.MD0[:], T.QF[:, 0:1], None, A.is_equal), [("MD0", 0, 128), ("QF", 0, 1)], [("MD", 0, 128)])
    op("v", ts(T.IV[:], T.IV0[:], T.GF[:, 0:1], None, A.add), [("IV0", 0, 128), ("GF", 0, 1)], [("IV", 0, 128)])
    op("v", ts(T.REV[:], T.QM[:], -1.0, 127.0, A.mult, A.add), [("QM", 0, 8)], [("REV", 0, 8)])
    for m in range(8):
        op("v", ts(T.KM[:, 128 * m:128 * m + 128], T.PL0[:], T.QM[:, m:m + 1], None, A.is_gt), [("PL0", 0, 128), ("QM", 0, 8)], [("KM", 128 * m, 128 * m + 128)])

    partners = [T.cores[rank ^ (1 << t)] for t in range(ROUNDS)]
    common = [e for e in topo.engines(core, partners[0]) if all(e in topo.engines(core, p) for p in partners)]
    mask, ne = sum(1 << e for e in common), len(common)
    nout = ROUNDS + 7

    def send(t, land, src, arr, reads):
        deps("g", reads, [])
        rid, pid = topo.addr(partners[t])[:2]
        total["sent"] = total.get("sent", 0) + ne
        g.remote_dma(land, src, T.sem[arr], T.sem.sent, pid, rid, mask)
        total[arr] = ne

    for t in range(ROUNDS):
        QH, SH, QUR, SUR = T["QH%d" % t], T["SH%d" % t], T["QUR%d" % t], T["SUR%d" % t]
        nQH, nSH = "QH%d" % t, "SH%d" % t
        ru = [("QUR%d" % t, 0, 128), ("SUR%d" % t, 0, 128)]

        def gather(e, el, lo, hi):
            out = T.H[:, 4 * lo + el:4 * hi:4]
            if t == 0:
                win = T.XI[:, 0:2048].indirect(T.OFH[:, 64 * el + lo // 16:64 * el + hi // 16])
                reads = [("XI", 0, 2048), ("OFH", 64 * el, 64 * el + 64)]
            else:
                win = T["XP%d" % el][:, 0:512].indirect(T.OFP[:, lo // 16:hi // 16])
                reads = [("XP%d" % el, 0, 512), ("OFP", 0, 64)]
            op(e, cp(out, win) if e == "v" else act(out, win, ACT.Copy), reads, [("H.%d" % el, lo, hi)])

        def quant(a, b):
            op("v", lambda: V.quantize_mx(QH[:, a:b], SH[:, a:b], T.H[:, 4 * a:4 * b]),
               [("H.%d" % e, a, b) for e in range(4)], [(nQH, a, b), (nSH, a, b)])

        def rows(h, base):
            a = 512 * h
            op("t", mm(T.psR[:, base + a:base + a + 512], QUR[:, 0:128], SUR[:, 0:128], QH[:, a:a + 512], SH[:, a:a + 512]),
               ru + [(nQH, a, a + 512), (nSH, a, a + 512)], [("psR", base + a, base + a + 512)])

        def cols(c):
            k = c % 4
            op("t", mm(T.psC[:, 512 * k:512 * k + 128], QH[:, 128 * c:128 * c + 128], SH[:, 128 * c:128 * c + 128], QUR[:, 0:128], SUR[:, 0:128]),
               ru + [(nQH, 128 * c, 128 * c + 128), (nSH, 128 * c, 128 * c + 128)], [("psC", 512 * k, 512 * k + 512)])

        if t == 0:
            first = [("v", 0), ("s", 2), ("v", 1), ("s", 3)]
            second = [("s", 2, 512, 1024), ("s", 3, 512, 1024), ("v", 0, 512, 1024), ("s", 1, 768, 1024), ("v", 1, 512, 768)]
        else:
            first = [("s", 0), ("s", 1), ("v", 2), ("v", 3)]
            second = [("s", 0, 512, 1024), ("s", 1, 512, 1024), ("s", 2, 512, 1024), ("v", 3, 512, 768), ("s", 3, 768, 1024)]
        for e, el in first:
            gather(e, el, 0, 512)
        quant(0, 512)
        for e, el, lo, hi in second:
            gather(e, el, lo, hi)
        for c in range(4):
            cols(c)
        quant(512, 768)
        quant(768, 1024)
        rows(0, 0)
        rows(0, 1024)
        op("v", cp(T.CC[:, 0:4], T.psC[:, 0:2048:512]), [("psC", 0, 2048)], [("CC", 0, 4)])
        op("v", ts(T.NCC[:, 0:2], T.CC[:, 0:2], -1.0, None, A.mult), [("CC", 0, 2)], [("NCC", 0, 2)])
        rows(1, 0)
        for c in range(4, 8):
            cols(c)
        rows(1, 1024)

        def sign(i, h):
            c = SCH[i]
            op("s", act(T["SG%d" % c][:, 8 + 512 * h:520 + 512 * h], T.psR[:, 1024 + 512 * h:1536 + 512 * h], ACT.Sign, bias=T.NCC[:, i:i + 1]),
               [("psR", 1024 + 512 * h, 1536 + 512 * h), ("NCC", i, i + 1)], [("SG%d" % c, 8 + 512 * h, 520 + 512 * h)])

        def triangles(i):
            c = SCH[i]
            sg, nm, d = T["SG%d" % c], "SG%d" % c, 8 + 128 * c
            op("g", lambda: g.affine_select(sg[:, 1032:1160], sg[:, d:d + 128], [[1, 128]], A.is_gt, 0.0, 0, -1),
               [(nm, d, d + 128)], [(nm, 1032, 1160)])
            op("g", lambda: g.affine_select(sg[:, d:d + 128], sg[:, d:d + 128], [[-1, 128]], A.is_gt, 0.0, 0, 1),
               [(nm, d, d + 128)], [(nm, d, d + 128)])

        def eq(c):
            cb = T["CB%d" % c]
            op("v", ts(T.EQR[:, 128 * c:128 * c + 128], T.psR[:, 128 * c:128 * c + 128], T.CC[:, c:c + 1], None, A.is_equal),
               [("psR", 128 * c, 128 * c + 128), ("CC", c, c + 1)], [("EQR", 128 * c, 128 * c + 128)])
            op("g", lambda: g.affine_select(cb[:, 1024:1152], T.EQR[:, 128 * c:128 * c + 128], [[1, 128]], A.is_gt, 0.0, 0, -1),
               [("EQR", 128 * c, 128 * c + 128)], [("CB%d" % c, 1024, 1152)])

        def beat(c, a, b, o):
            op("v", ts(T["CB%d" % c][:, a:b], T.psR[:, a:b], T.CC[:, c:c + 1], None, o),
               [("psR", a, b), ("CC", c, c + 1)], [("CB%d" % c, a, b)])

        def total_of(i):
            cb = T["CB%d" % VCH[i]]
            op("v", scan(T.SCB[:, 576 * i:576 * i + 576], cb[:, 0:576], cb[:, 576:1152], A.add, A.add),
               [("CB%d" % VCH[i], 0, 1152)], [("SCB", 576 * i, 576 * i + 576)])

        for i in (0, 1):
            sign(i, 0)
            triangles(i)
        for c in (2, 3):
            eq(c)
        beat(2, 0, 384, A.is_lt)
        beat(2, 384, 512, A.is_le)
        beat(3, 0, 512, A.is_lt)
        op("v", ms(T.WIN[:, 896:1024], 0.0), [], [("WIN", 896, 1024)])
        op("v", cp(T.CC[:, 4:8], T.psC[:, 0:2048:512]), [("psC", 0, 2048)], [("CC", 4, 8)])
        op("v", ts(T.NCC[:, 2:3], T.CC[:, 7:8], -1.0, None, A.mult), [("CC", 7, 8)], [("NCC", 2, 3)])
        for i, h in ((2, 0), (2, 1), (0, 1), (1, 1)):
            sign(i, h)
        triangles(2)
        for i, c in enumerate(SCH):
            sg, nm, d, j = T["SG%d" % c], "SG%d" % c, 136 + 128 * c, 1160 * i
            op("s", act(T.JNK[:, j + 6:j + d], sg[:, 6:d], ACT.Relu, scale=-1.0, accum_out=T.APR[:, i:i + 1]),
               [(nm, 6, d)], [("APR", i, i + 1), ("JNK", j + 6, j + d)])
            op("s", act(T.JNK[:, j + d:j + 1160], sg[:, d:1160], ACT.Relu, accum_out=T.ASU[:, i:i + 1]),
               [(nm, d, 1160)], [("ASU", i, i + 1), ("JNK", j + d, j + 1160)])
        if t == 0:
            op("s", act(T.FVN[:], T.FVP[:].indirect(T.POSL[:, 0:64]), ACT.Copy),
               [("FVP.%d" % q, 0, 1024) for q in range(16)] + [("POSL", 0, 64)], [("FVN", 0, 1024)])
        beat(2, 512, 1024, A.is_le)
        eq(4)
        beat(3, 512, 1024, A.is_le)
        total_of(0)
        for i in (2, 3, 4):
            c = VCH[i]
            if i > 2:
                eq(c)
            beat(c, 0, 128 * c + 128, A.is_lt)
            beat(c, 128 * c + 128, 1024, A.is_le)
            total_of(i - 1)
        total_of(4)
        op("v", cp(T.OFR[:, 0:5], T.SCB[:, 575:2880:576]), [("SCB", 0, 2880)], [("OFR", 0, 5)])
        op("v", tt(T.OFR[:, 5:8], T.APR[:, 0:3], T.ASU[:, 0:3], A.subtract), [("ASU", 0, 3), ("APR", 0, 3)], [("OFR", 5, 8)])
        op("v", cp(T.WIN[:, 0:1024].indirect(T.OFR[:, 0:8]), T.IV[:]), [("OFR", 0, 8), ("IV", 0, 128)], [("WIN", 0, 1024)])
        op("v", lambda: V.transpose(T.TT[:, 0:128], T.WIN[:, 896:1024]), [("WIN", 896, 1024)], [("TT.0", 0, 128)])
        op("v", lambda: V.transpose(T.TT[:, 128:288], T.WIN[:, 880:1040]), [("WIN", 880, 1040)], [("TT.1", 0, 160)])
        op("v", tt(T.SA[:, 0:9], T.TT[:, 0:288:32], T.TT[:, 16:288:32], A.add), [("TT.0", 0, 128), ("TT.1", 0, 160)], [("SA", 0, 9)])
        op("v", tt(T.SB[0:64, 0:9], T.SA[0:64, 0:9], T.SA[64:128, 0:9], A.add), [("SA", 0, 9)], [("SB", 0, 9)])
        op("v", tt(T.SC[0:32, 0:9], T.SB[0:32, 0:9], T.SB[32:64, 0:9], A.add), [("SB", 0, 9)], [("SC", 0, 9)])
        op("v", cp(T.SC[32:64, 0:9], T.SC[0:32, 0:9]), [("SC", 0, 9)], [("SC", 0, 9)])
        op("v", cp(T.SC[64:128, 0:9], T.SC[0:64, 0:9]), [("SC", 0, 9)], [("SC", 0, 9)])
        LST, nL = T["LST%d" % t], "LST%d" % t
        op("v", tt(T.PP[:, 0:9], T.SC[:, 0:9], T.MK[:, 0:9], A.mult), [("SC", 0, 9), ("MK", 0, 18)], [("PP", 0, 9)])
        op("v", tt(T.PP[:, 9:18], T.SC[:, 0:9], T.MK[:, 9:18], A.mult), [("SC", 0, 9), ("MK", 0, 18)], [("PP", 9, 18)])
        op("v", tt(LST[:, 0:8:2], T.PP[:, 0:4], T.PP[:, 4:8], A.add), [("PP", 0, 9)], [(nL + ".0", 0, 8)])
        op("v", tt(LST[:, 1:8:2], T.PP[:, 9:13], T.PP[:, 14:18], A.add), [("PP", 9, 18)], [(nL + ".1", 0, 8)])
        rL = [(nL + ".0", 0, 8), (nL + ".1", 0, 8)]

        send(t, T["LR%d" % t][:], LST[:], "arrL%d" % t, rL)
        op("v", cp(T["SL%d" % t][:, 0:128].bitcast(dt.uint32), QH[:, 0:1024].bitcast(dt.uint32).indirect(LST[:, 0:8])),
           [(nQH, 0, 1024)] + rL, [("SL%d" % t, 0, 128)])
        op("s", act(T["SS%d" % t][:, 0:128], SH[:, 0:1024].indirect(LST[:, 0:8]), ACT.Copy),
           [(nSH, 0, 1024)] + rL, [("SS%d" % t, 0, 128)])
        send(t, T["LC%d" % t][:, 0:128].bitcast(dt.uint8), T["SL%d" % t][:, 0:128].bitcast(dt.uint8), "arrC%d" % t, [("SL%d" % t, 0, 128)])
        send(t, T["LS%d" % t][:, 0:128], T["SS%d" % t][:, 0:128], "arrS%d" % t, [("SS%d" % t, 0, 128)])
        note("a", ("arrL%d" % t, ne), [], [("LR%d" % t, 0, 8)])
        note("a", ("arrC%d" % t, ne), [], [("LC%d" % t, 0, 128)])
        note("a", ("arrS%d" % t, ne), [], [("LS%d" % t, 0, 128)])
        FLS, nF = T["FLS%d" % t], "FLS%d" % t
        op("s", act(T.FR[:], T.IOT[:].indirect(LST[:, 0:8]), ACT.Copy), [("IOT", 0, 1024)] + rL, [("FR", 0, 128)])
        op("s", act(FLS[:], T.FR[:].indirect(T.REV[:, 0:8]), ACT.Copy), [("FR", 0, 128), ("REV", 0, 8)], [(nF, 0, 128)])
        dma("y", T.fl[t:t + 1, :], FLS[0:1, :], "dout", nout, [(nF, 0, 128)], [])
        if t == 0:
            for e in range(4):
                op("v", cp(T["XP%d" % e][:, 0:512], T.XI[:, e:2048:4]), [("XI", 0, 2048)], [("XP%d" % e, 0, 512)])
            lay_u(1)
        if t == 1:
            lay_u(2)
            op("v", lambda: V.quantize_mx(T.QWY[:, 0:128], T.SWY[:, 0:128], T.WYB[:, 0:512]), [("WYB", 0, 512)], [("QWY", 0, 128), ("SWY", 0, 128)])
        if t == 2:
            for e in range(4):
                op("v", cp(T.XF[:, e:2048:4], T["XP%d" % e][:, 0:512]), [("XP%d" % e, 0, 512)], [("XF.%d" % e, 0, 4096)])

        LR, nR = T["LR%d" % t], "LR%d" % t
        op("v", tt(T.VM[:], T.FVN[:].indirect(LR[:, 0:8]), T.MD[:], A.mult), [("FVN", 0, 1024), (nR, 0, 8), ("MD", 0, 128)], [("VM", 0, 128)])
        op("s", act(T.VRO[:], T.FVN[:].indirect(LR[:, 0:8]), ACT.Copy), [("FVN", 0, 1024), (nR, 0, 8)], [("VRO", 0, 128)])
        op("v", scan(T.VC[:, 16:144], T.VM[:], T.ZR[:], A.add, A.add), [("VM", 0, 128), ("ZR", 0, 128)], [("VC", 16, 144)])
        op("v", tt(T.OFG[:], T.VC[:, 31:144:16], T.VC[:, 15:128:16], A.subtract), [("VC", 0, 144)], [("OFG", 0, 8)])
        op("v", tt(T.VW[:], T.VC[:, 31:144:16], T.VC[:, 15:128:16], A.subtract), [("VC", 0, 144)], [("VW", 0, 8)])
        for e in range(4):
            op("s", act(T.OLD[:, 128 * e:128 * e + 128], T["XP%d" % e][:, 0:512].indirect(T.OFG[:, 0:8]), ACT.Copy, scale=32.0),
               [("XP%d" % e, 0, 512), ("OFG", 0, 8)], [("OLD", 128 * e, 128 * e + 128)])
        for m in range(8):
            a = 128 * m
            op("v", ts(T.EQ[:, a:a + 128], T.VRO[:], T.VW[:, m:m + 1], 512.0, A.is_equal, A.mult),
               [("VRO", 0, 128), ("VW", 0, 8)], [("EQ", a, a + 128)])
        op("v", scan(T.LOS[:], T.EQ[:], T.KM[:], A.add, A.mult), [("EQ", 0, 1024), ("KM", 0, 1024)], [("LOS", 0, 1024)])
        if t < 2:
            op("v", tt(T.OFS[:], T.LOS[:, 127:1024:128], T.VW[:], A.add), [("LOS", 0, 1024), ("VW", 0, 8)], [("OFS", 0, 8)])
        else:
            op("v", tt(T.VD[:], T.LOS[:, 127:1024:128], T.VW[:], A.add), [("LOS", 0, 1024), ("VW", 0, 8)], [("VD", 0, 8)])
            for e in range(4):
                op("v", ts(T.OFX[:, 8 * e:8 * e + 8], T.VD[:], 4.0, float(e), A.mult, A.add), [("VD", 0, 8)], [("OFX", 8 * e, 8 * e + 8)])

        for b in range(4):
            op("t", mm(T.psC[:, 512 * b:512 * b + 128], T.WQ[:, 128 * b:128 * b + 128], T.WSC[:, 128 * b:128 * b + 128],
                       T["LC%d" % t][:, 0:128], T["LS%d" % t][:, 0:128]),
               [("WQ", 0, 512), ("WSC", 0, 512), ("LC%d" % t, 0, 128), ("LS%d" % t, 0, 128)], [("psC", 512 * b, 512 * b + 512)])
        for b in range(4):
            a = 128 * b
            op("v", tt(T.TMP[:, a:a + 128], T.psC[:, 512 * b:512 * b + 128], T.OLD[:, a:a + 128], A.add),
               [("psC", 512 * b, 512 * b + 128), ("OLD", a, a + 128)], [("TMP", a, a + 128)])
            op("s", act(T.NV[:, a:a + 128], T.TMP[:, a:a + 128], ACT.Copy, scale=1.0 / 64), [("TMP", a, a + 128)], [("NV", a, a + 128)])
        for b in range(4):
            if t < 2:
                op("v", cp(T["XP%d" % b][:, 0:1024].indirect(T.OFS[:, 0:8]), T.NV[:, 128 * b:128 * b + 128]),
                   [("OFS", 0, 8), ("NV", 128 * b, 128 * b + 128)], [("XP%d" % b, 0, 1024)])
            else:
                op("v", cp(T.XF[:, 0:4096].indirect(T.OFX[:, 8 * b:8 * b + 8]), T.NV[:, 128 * b:128 * b + 128]),
                   [("OFX", 0, 32), ("NV", 128 * b, 128 * b + 128)], [("XF.%d" % e, 0, 4096) for e in range(4)])

    for h in range(2):
        a = 256 * h
        op("v", lambda: V.quantize_mx(T.QX[:, a:a + 256], T.SX[:, a:a + 256], T.XF[:, 4 * a:4 * a + 1024]),
           [("XF.%d" % e, 0, 4096) for e in range(4)], [("QX", a, a + 256), ("SX", a, a + 256)])
        op("t", mm(T.psR[:, 1024 * h:1024 * h + 256], T.QWY[:, 0:128], T.SWY[:, 0:128], T.QX[:, a:a + 256], T.SX[:, a:a + 256]),
           [("QWY", 0, 128), ("SWY", 0, 128), ("QX", a, a + 256), ("SX", a, a + 256)], [("psR", 1024 * h, 1024 * h + 512)])
    op("s", act(T.YS[:, 0:256], T.psR[:, 0:256], ACT.Copy), [("psR", 0, 256)], [("YS", 0, 256)])
    op("v", cp(T.YS[:, 256:512], T.psR[:, 1024:1280]), [("psR", 1024, 1280)], [("YS", 256, 512)])
    dma("y", T.oc[:, 0:2048], T.QX[:, 0:512].bitcast(dt.uint8), "dout", nout, [("QX", 0, 512)], [])
    dma("s", T.y[:, 0:256], T.YS[:, 0:256], "dout", nout, [("YS", 0, 256)], [])
    dma("y", T.y[:, 256:512], T.YS[:, 256:512], "dout", nout, [("YS", 256, 512)], [])
    for k in range(4):
        dma("y" if k % 2 else "s", T.osc[4 * k:4 * k + 4, :], T.SX[32 * k:32 * k + 4, 0:512], "dout", nout, [("SX", 0, 512)], [])
    for sem in sorted(total):
        if most.get(sem, 0) < total[sem]:
            need("g", (sem, total[sem]))
